import numpy as np
import ml_dtypes


def mxq(x, axis, fmt="e4m3"):
    dtype, down = {"e4m3": (ml_dtypes.float8_e4m3fn, 7), "e5m2": (ml_dtypes.float8_e5m2, 14)}[fmt]
    v = np.moveaxis(np.asarray(x, np.float32).astype(ml_dtypes.bfloat16).astype(np.float64), axis, -1)
    blocks = v.reshape(v.shape[:-1] + (-1, 32))
    amax = np.abs(blocks).max(-1, keepdims=True)
    byte = np.maximum(np.where(amax > 0, np.frexp(amax)[1] - 1 + 127, 0) - down, 1)
    scale = np.exp2(byte - 127.0)
    codes = (blocks / scale).astype(np.float32).astype(dtype).astype(np.float64)
    return np.moveaxis((codes * scale).reshape(v.shape), -1, axis)


WIDE = False


def mx_kscale(k):
    if not WIDE:
        return np.ones(k)
    levels = np.array([10, -10, 5, -5, 0])
    if k % 512:
        return np.exp2(np.random.permutation(np.resize(levels, k // 32))).repeat(32)
    a = np.empty((k // 512, 16))
    for p in range(k // 512):
        a[p, :8] = np.random.permutation(np.resize(levels, 8))
        for g in range(8):
            far = levels[np.abs(levels - a[p, g]) >= 10]
            a[p, g + 8] = far[np.random.randint(len(far))]
    return np.exp2(a.ravel()).repeat(32)


BF16 = ml_dtypes.bfloat16


def bf(x):
    return np.asarray(x, np.float32).astype(BF16)


def f64(x):
    return np.asarray(x).astype(np.float64)


E2M1 = np.array([0.0, 0.5, 1.0, 1.5, 2.0, 3.0, 4.0, 6.0, -0.0, -0.5, -1.0, -1.5, -2.0, -3.0, -4.0, -6.0])


def pack_weight(w, fmt):
    k, n = w.shape
    w = f64(bf(w)).reshape(k // 32, 32, n)
    amax = np.abs(w).max(1)
    if fmt == "e4m3":
        byte = np.frexp(amax)[1] - 1 + 127 - 7
    else:
        mant, ex = np.frexp(amax / 6.0)
        byte = np.where(mant > 0.5, ex, ex - 1) + 127
    byte = np.clip(np.where(amax > 0, byte, 1), 1, 254)
    scaled = (w * np.exp2(127.0 - byte)[:, None, :]).reshape(k, n).astype(np.float32)
    by_word = np.ascontiguousarray(scaled.reshape(k // 512, 128, 4, n).transpose(0, 1, 3, 2))
    if fmt == "e4m3":
        words = by_word.astype(ml_dtypes.float8_e4m3fn).view(np.uint8)
    else:
        c = by_word.astype(ml_dtypes.float4_e2m1fn).view(np.uint8) & 0xF
        words = c[..., 0::2] | (c[..., 1::2] << 4)
    return np.ascontiguousarray(words), np.ascontiguousarray(byte.astype(np.uint8).reshape(k // 512, 16, n))


def unpack_weight(words, scales, fmt):
    g, p, n, _ = words.shape
    if fmt == "e4m3":
        vals = np.ascontiguousarray(words).view(ml_dtypes.float8_e4m3fn).astype(np.float64)
    else:
        nib = np.empty((g, p, n, 4), np.uint8)
        nib[..., 0::2] = words & 0xF
        nib[..., 1::2] = words >> 4
        vals = E2M1[nib]
    vals = vals * np.repeat(np.exp2(scales.astype(np.float64) - 127.0), 8, axis=1)[..., None]
    return vals.transpose(0, 1, 3, 2).reshape(g * 512, n)


B, S, H, C, E = 2, 1024, 512, 256, 512


def logsumexp(v, axis):
    m = v.max(axis=axis, keepdims=True)
    return m + np.log(np.sum(np.exp(v - m), axis=axis, keepdims=True))


def sinkhorn_step(l, lm):
    l = l - logsumexp(l, 2)
    l = l - logsumexp(l, 1) + lm[None, None, :]
    return l


def draw0():
    s, u = mx_kscale(H), mx_kscale(S)
    h = bf(np.random.standard_normal((B, S, H)) * s)
    wp_words, wp_scales = pack_weight(np.random.standard_normal((H, C)) / np.sqrt(H) / s[:, None], "e4m3")
    return {
        "h": h,
        "wp_words": wp_words,
        "wp_scales": wp_scales,
        "z": bf(np.log(C) + 1.5 * np.random.standard_normal((B, S))),
        "g": bf(0.03 * np.random.standard_normal((B, S)) * u),
        "f": bf(0.02 * np.random.standard_normal((B, S, E)) / u[:, None]),
    }


def core(h, wp_words, wp_scales, z, g, f):
    h, z, g, f = f64(h), f64(z), f64(g), f64(f)
    wp = unpack_weight(wp_words, wp_scales, "e4m3")
    s = h.shape[1]
    c = wp.shape[1]

    t = mxq(h, 2, "e4m3") @ wp

    l = np.concatenate([t, z[:, :, None]], axis=-1)

    lm = np.concatenate([np.zeros(c), np.full(1, np.log(s - c))])

    for _ in range(2):
        l = sinkhorn_step(l, lm)

    pg = np.exp(l[:, :, :c]) * g[:, :, None] * np.sqrt(s)

    v = mxq(pg, 1, "e4m3").transpose(0, 2, 1) @ mxq(f, 1, "e4m3")

    y = v / np.sqrt(np.mean(v * v, axis=-1, keepdims=True) + 1e-6)
    return y


def e4m3fn_bytes(y):
    return np.clip(np.asarray(y, np.float64), -448.0, 448.0).astype(np.float32).astype(ml_dtypes.float8_e4m3fn).view(np.uint8)


def e4m3fn_values(b):
    return np.asarray(b, np.uint8).view(ml_dtypes.float8_e4m3fn).astype(np.float64)


def setup_inputs():
    d = draw0()
    x0 = np.asarray(d['h']).astype(np.float64)
    s = (np.max(np.abs(x0), axis=(0, 1), keepdims=True) / 448.0).astype(np.float32)
    out = {}
    for k, v in d.items():
        if k == 'h':
            out['h_bytes'] = e4m3fn_bytes(x0 / s.astype(np.float64))
            out['h_scale'] = s
        else:
            out[k] = v
    return out


def reference(h_bytes, h_scale, wp_words, wp_scales, z, g, f):
    return core(e4m3fn_values(h_bytes) * h_scale.astype(np.float64), wp_words, wp_scales, z, g, f)

@@ -1,0 +1,513 @@
+from contextlib import ExitStack
+
+import concourse.mybir as mybir
+from concourse.masks import make_identity
+
+B, S, H, C, E = 2, 1024, 512, 256, 512
+FLOPS = 2 * B * S * H * C + 2 * B * C * S * E
+
+F32 = mybir.dt.float32
+BF16 = mybir.dt.bfloat16
+U32 = mybir.dt.uint32
+I32 = mybir.dt.int32
+U8 = mybir.dt.uint8
+FP8 = mybir.dt.float8_e4m3fn
+FP8X4 = mybir.dt.float8_e4m3fn_x4
+ALU = mybir.AluOpType
+ACT = mybir.ActivationFunctionType
+AX = mybir.AxisListType
+
+P = 128
+BANK = 512
+TILES = S // P
+GROUPS = S // 256
+HALVES = C // P
+PASSES = S // 512
+SUM_N = 48
+ROW = 264
+
+
+def tile_saladsinkhorndustbinaggregation_w8_kernel(tc, h_bytes, h_scale, wp_words, wp_scales, z, g, f, out):
+    nc = tc.nc
+    with ExitStack() as ctx:
+        keep = ctx.enter_context(tc.tile_pool(name="keep", bufs=1))
+        stage = ctx.enter_context(tc.tile_pool(name="stage", bufs=4))
+        psum = ctx.enter_context(tc.psum_pool(name="psum", bufs=1))
+        ctx.enter_context(tc.manual_schedule())
+
+        def bank(name, number):
+            return psum.tile([P, BANK], F32, name=name, tag="bank_%d" % number)
+
+        def kept(name, shape, dtype):
+            return keep.tile(shape, dtype, name=name, align_bytes=64)
+
+        both = range(B)
+        ident = kept("ident", [P, P], F32)
+        ones = kept("ones", [P, P], F32)
+        inv_root = kept("inv_root", [P, 1], F32)
+        z_rows = kept("z_rows", [P, P], BF16)
+        neg_z_rows = kept("neg_z_rows", [P, P], F32)
+        hs = kept("hs", [P, 2 * H], F32)
+        h_first = kept("hbytes_first", [P, 1, 2 * H], U8)
+        h_rest = kept("hbytes_rest", [P, GROUPS - 1, 2 * H], U8)
+        h_second = kept("hbytes_second", [P, GROUPS, 2 * H], U8)
+        hbytes = [[h_first[:, 0, :]] + [h_rest[:, q, :] for q in range(GROUPS - 1)], [h_second[:, q, :] for q in range(GROUPS)]]
+        w_codes = kept("w_codes", [P, C], U32)
+        w_scales = kept("w_scales", [P, C], U8)
+        f_raw = [[kept("f_raw_%d_%d" % (b, a), [P, 4, E], BF16) for a in range(PASSES)] for b in both]
+        f_codes = [[kept("f_codes_%d_%d" % (b, a), [P, E], U32) for a in range(PASSES)] for b in both]
+        f_scales = [[kept("f_scales_%d_%d" % (b, a), [P, E], U8) for a in range(PASSES)] for b in both]
+        gate = [kept("gate_%d" % b, [P, S], BF16) for b in both]
+        neg_all = kept("neg_l", [P, B * TILES, ROW], F32)
+        neg_l = [neg_all[:, b * TILES : (b + 1) * TILES, :] for b in both]
+        dust_cost = kept("dust_cost", [P, B * TILES], F32)
+        dust_exp = kept("dust_exp", [P, B * TILES], F32)
+        dust_min_p = kept("dust_min_p", [P, B], F32)
+        dust_min = kept("dust_min", [P, B], F32)
+        dust_sum_p = kept("dust_sum_p", [P, B], F32)
+        dust_inv = kept("dust_inv", [P, B], F32)
+        neg_max = kept("neg_max", [P, B * TILES], F32)
+        row_sum = kept("row_sum", [P, B * TILES], F32)
+        log_sum = kept("log_sum", [P, B * TILES], F32)
+        lse = kept("lse", [P, B * TILES], F32)
+        cost = [[kept("cost_%d_%d" % (b, hf), [P, S], F32) for hf in range(HALVES)] for b in both]
+        small = {}
+        for b in both:
+            for name, width in (("cmin", 4), ("col1", 2), ("v1", 2), ("dust", 8), ("row2", 8), ("u2", 8), ("col2p", 4), ("col2", 2),
+                                ("v2", 2), ("ss", 2), ("ms", 2), ("rs", 2)):
+                small[name, b] = kept("%s_%d" % (name, b), [P, width], F32)
+
+        nc.scalar.dma_start(out=z_rows[0 : B * TILES, :], in_=z.rearrange("b (j m) -> (b j) m", m=P))
+        nc.sync.dma_start(out=hs[:, 0:H], in_=h_scale.rearrange("a o k -> (a o k)").partition_broadcast(P))
+
+        def load_h(dst, b, q0, q1):
+            rows = h_bytes[b, 256 * q0 : 256 * q1, :]
+            nc.sync.dma_start(out=dst[:], in_=rows.rearrange("(q m e) k -> m q (e k)", m=P, e=2))
+
+        def load_f(b, a):
+            rows = f[b, 512 * a : 512 * (a + 1), :]
+            nc.sync.dma_start(out=f_raw[b][a][:], in_=rows.rearrange("(p t) e -> p t e", t=4))
+
+        nc.gpsimd.memset(w_scales[:].bitcast(I32), 0)
+        make_identity(nc, ident[:])
+        nc.gpsimd.memset(neg_z_rows[:], 0.0)
+        nc.gpsimd.memset(ones[:], 1.0)
+
+        load_h(h_first, 0, 0, 1)
+        load_h(h_rest, 0, 1, GROUPS)
+        nc.sync.dma_start(
+            out=w_codes[:].bitcast(I32), in_=wp_words[0].rearrange("p n t -> p (n t)").bitcast(I32)
+        )
+        for quad in range(4):
+            nc.sync.dma_start(
+                out=w_scales[32 * quad : 32 * quad + 4, :].bitcast(I32),
+                in_=wp_scales[0, 4 * quad : 4 * quad + 4, :].bitcast(I32),
+            )
+        load_h(h_second, 1, 0, GROUPS)
+        for b in both:
+            for a in range(PASSES):
+                load_f(b, a)
+        for b in both:
+            nc.sync.dma_start(out=gate[b][:], in_=g[b].partition_broadcast(P))
+
+        held = {}
+        def dustbin_scores():
+            nc.scalar.activation(out=neg_z_rows[0 : B * TILES, :], in_=z_rows[0 : B * TILES, :], func=ACT.Copy, scale=-1.0)
+            z_bank = bank("z_bank", 4)
+            nc.tensor.transpose(z_bank[:, 0:P], neg_z_rows[:], ident[:])
+            held["z"] = z_bank
+
+        def dustbin_column():
+            nc.vector.tensor_copy(out=neg_all[:, :, C], in_=held["z"][:, 0 : B * TILES])
+
+
+        def widen(b, q, pieces):
+            hb = stage.tile([P, 2 * H], BF16, name="hb", align_bytes=64)
+            width = 2 * H // pieces
+            for e in range(pieces):
+                cols = slice(e * width, (e + 1) * width)
+                nc.vector.tensor_tensor(out=hb[:, cols], in0=hbytes[b][q][:, cols].bitcast(FP8), in1=hs[:, 0:width], op=ALU.mult)
+            held["hb", b, q] = hb
+
+        def turn_h(b, q):
+            hb = held["hb", b, q]
+            words = hb[:].bitcast(F32)
+            turned = bank("turned", q % 2)
+            for e in range(2):
+                for u in range(2):
+                    r = 2 * e + u
+                    nc.tensor.transpose(turned[:, r * P : (r + 1) * P], words[:, 256 * e + u : 256 * (e + 1) : 2], ident[:])
+            held["turned", b, q] = turned
+
+        def group_h(b, q):
+            turned = held["turned", b, q]
+            grouped = stage.tile([P, 1024], BF16, name="grouped", align_bytes=64)
+            nc.scalar.copy(
+                out=grouped[:].bitcast(F32).rearrange("p (m r) -> p m r", r=4),
+                in_=turned[:].rearrange("p (r m) -> p m r", r=4),
+            )
+            held["grouped", b, q] = grouped
+
+        def scores(b, q):
+            codes = stage.tile([P, 256], U32, name="h_codes", align_bytes=64)
+            scales = stage.tile([P, 256], U8, name="h_scales", align_bytes=64)
+            nc.vector.quantize_mx(out=codes[:].bitcast(FP8X4), scales=scales[:], in_=held["grouped", b, q][:])
+            t_bank = bank("t_bank", 2 + q % 2)
+            for i in range(2):
+                cols = slice(i * P, (i + 1) * P)
+                nc.tensor.matmul_mx(
+                    out=t_bank[:, i * C : (i + 1) * C],
+                    lhsT=codes[:, cols].bitcast(FP8X4),
+                    lhsT_scale=scales[:, cols],
+                    rhs=w_codes[:].bitcast(FP8X4),
+                    rhs_scale=w_scales[:],
+                    start=True,
+                    stop=True,
+                )
+            held["t", b, q] = t_bank
+
+        def empty_scores(b, q):
+            t_bank = held["t", b, q]
+            nc.scalar.activation(
+                out=neg_l[b][:, 2 * q : 2 * q + 2, 0:C], in_=t_bank[:].rearrange("p (i c) -> p i c", i=2), func=ACT.Copy, scale=-1.0
+            )
+
+        def row_max(b, q):
+            n = b * TILES + 2 * q
+            nc.vector.tensor_reduce(
+                out=neg_max[:, n : n + 2], in_=neg_l[b][:, 2 * q : 2 * q + 2, 0 : C + 1], axis=AX.X, op=ALU.min
+            )
+
+        def empty_scores_and_max(b, q):
+            for i in range(2):
+                j = 2 * q + i
+                n = b * TILES + j
+                nc.vector.tensor_scalar(
+                    out=neg_l[b][:, j, 0:C], in0=held["t", b, q][:, i * C : (i + 1) * C], scalar1=-1.0,
+                    scalar2=neg_l[b][:, j, C : C + 1], op0=ALU.mult, op1=ALU.min, accum_out=neg_max[:, n : n + 1],
+                )
+
+        def row_exp(b, q):
+            for j in (2 * q, 2 * q + 1):
+                n = b * TILES + j
+                junk = stage.tile([P, C + 1], BF16, name="junk_row")
+                nc.scalar.activation(
+                    out=junk[:], in_=neg_l[b][:, j, 0 : C + 1], func=ACT.Exp, scale=-1.0, bias=neg_max[:, n : n + 1],
+                    accum_out=row_sum[:, n : n + 1],
+                )
+
+        def interleave_f(b, a, engine, part=0, parts=1):
+            if part == 0:
+                held["fi", b, a] = kept("f_grouped_%d_%d" % (b, a), [P, E, 4], BF16)
+            cols = slice(part * E // parts, (part + 1) * E // parts)
+            dst = held["fi", b, a][:, cols, :].rearrange("p (c i) t -> p c t i", i=4)
+            src = f_raw[b][a][:, :, cols].rearrange("p t (c i) -> p c t i", i=4)
+            if engine == "scalar":
+                nc.scalar.copy(out=dst, in_=src)
+            else:
+                nc.vector.tensor_copy(out=dst, in_=src)
+
+        def quantize_f(b, a):
+            nc.vector.quantize_mx(
+                out=f_codes[b][a][:].bitcast(FP8X4), scales=f_scales[b][a][:],
+                in_=held["fi", b, a][:].rearrange("p c t -> p (c t)"),
+            )
+
+        def cost_bank_number(b, k, hf):
+            return (4 + 4 * b + 2 * k + hf) % 8
+
+        def turn_scores(b, k, hf):
+            nb = bank("cost_bank", cost_bank_number(b, k, hf))
+            for jj in range(4):
+                nc.tensor.matmul(
+                    out=nb[:, jj * P : (jj + 1) * P], lhsT=neg_l[b][:, 4 * k + jj, hf * P : (hf + 1) * P], rhs=ident[:],
+                    is_transpose=True, start=(jj == 0), stop=False,
+                )
+            held["n", b, k, hf] = nb
+
+        def add_lse(b, k, hf):
+            nb = held["n", b, k, hf]
+            for jj in range(4):
+                n = b * TILES + 4 * k + jj
+                nc.tensor.matmul(
+                    out=nb[:, jj * P : (jj + 1) * P], lhsT=lse[:, n : n + 1].to_broadcast([P, P]), rhs=ident[:],
+                    is_transpose=True, start=False, stop=(jj == 3),
+                )
+
+        def column_min(b, k, hf):
+            cmin = small["cmin", b]
+            nc.vector.tensor_scalar(
+                out=cost[b][hf][:, k * BANK : (k + 1) * BANK], in0=held["n", b, k, hf][:], scalar1=1.0,
+                scalar2=(None if k == 0 else cmin[:, hf : hf + 1]), op0=ALU.mult, op1=ALU.min,
+                accum_out=cmin[:, 2 * k + hf : 2 * k + hf + 1],
+            )
+
+        def dust_partition_min():
+            nc.vector.tensor_tensor(out=dust_cost[:], in0=lse[:], in1=neg_all[:, :, C], op=ALU.add)
+
+        def dust_partition_min2():
+            nc.vector.tensor_reduce(out=dust_min_p[:], in_=dust_cost[:].rearrange("p (b j) -> p b j", b=B), axis=AX.X, op=ALU.min)
+
+        def dust_spread(number):
+            db = bank("dust_bank", number)
+            for b in both:
+                nc.tensor.transpose(db[:, b * P : (b + 1) * P], dust_min_p[:, b : b + 1].to_broadcast([P, P]), ident[:])
+            held["dust"] = db
+
+        def dust_weights():
+            nc.vector.tensor_reduce(
+                out=dust_min[:], in_=held["dust"][:, 0 : B * P].rearrange("p (b m) -> p b m", b=B), axis=AX.X, op=ALU.min
+            )
+            for b in both:
+                cols = slice(b * TILES, (b + 1) * TILES)
+                nc.scalar.activation(
+                    out=dust_exp[:, cols], in_=dust_cost[:, cols], func=ACT.Exp, scale=-1.0, bias=dust_min[:, b : b + 1],
+                    accum_out=dust_sum_p[:, b : b + 1],
+                )
+
+        def dust_total(number):
+            db = bank("dust_sum_bank", number)
+            nc.tensor.matmul(out=db[:, 0:B], lhsT=ones[:], rhs=dust_sum_p[:], start=True, stop=True)
+            held["dust"] = db
+
+        def dust_mass():
+            nc.vector.reciprocal(out=dust_inv[:], in_=held["dust"][:, 0:B])
+            for b in both:
+                nc.gpsimd.tensor_scalar(
+                    out=small["dust", b][:], in0=dust_exp[:, b * TILES : (b + 1) * TILES], scalar1=dust_inv[:, b : b + 1],
+                    scalar2=float(S - C), op0=ALU.mult, op1=ALU.mult,
+                )
+
+        def column_exp(b, hf):
+            nc.scalar.activation(
+                out=cost[b][hf][:], in_=cost[b][hf][:], func=ACT.Exp, scale=-1.0,
+                bias=small["cmin", b][:, 2 + hf : 3 + hf], accum_out=small["col1", b][:, hf : hf + 1],
+            )
+
+        def column_inverse(b, hf):
+            nc.vector.reciprocal(out=small["v1", b][:, hf : hf + 1], in_=small["col1", b][:, hf : hf + 1])
+
+        def row_sums(b, hf, number):
+            if hf == 0:
+                held["rows", b] = bank("row_bank", number)
+            for j in range(TILES):
+                nc.tensor.matmul(
+                    out=held["rows", b][:, j * SUM_N : (j + 1) * SUM_N], lhsT=cost[b][hf][:, j * P : (j + 1) * P],
+                    rhs=small["v1", b][:, hf : hf + 1].to_broadcast([P, SUM_N]),
+                    start=(hf == 0 and j == 0), stop=(hf == HALVES - 1 and j == TILES - 1),
+                )
+
+        def row_total(b):
+            nc.vector.tensor_tensor(out=small["row2", b][:], in0=held["rows", b][:, 0 : TILES * SUM_N : SUM_N], in1=small["dust", b][:], op=ALU.add)
+
+        def row_inverse(b):
+            nc.vector.reciprocal(out=small["u2", b][:], in_=small["row2", b][:])
+
+        def row_spread(b, numbers):
+            for k in range(2):
+                ub = bank("u_bank", numbers[k])
+                for jj in range(4):
+                    j = 4 * k + jj
+                    nc.tensor.transpose(ub[:, jj * P : (jj + 1) * P], small["u2", b][:, j : j + 1].to_broadcast([P, P]), ident[:])
+                held["u", b, k] = ub
+
+        def column_sum(b, hf, k):
+            cols = slice(k * BANK, (k + 1) * BANK)
+            nc.vector.scalar_tensor_tensor(
+                out=cost[b][hf][:, cols], in0=cost[b][hf][:, cols], scalar=small["v1", b][:, hf : hf + 1],
+                in1=held["u", b, k][:], op0=ALU.mult, op1=ALU.mult,
+                accum_out=small["col2p", b][:, 2 * hf + k : 2 * hf + k + 1],
+            )
+
+        def column_total(b, hf):
+            c2 = small["col2p", b]
+            nc.vector.tensor_scalar(
+                out=small["col2", b][:, hf : hf + 1], in0=c2[:, 2 * hf : 2 * hf + 1], scalar1=c2[:, 2 * hf + 1 : 2 * hf + 2],
+                scalar2=inv_root[:], op0=ALU.add, op1=ALU.mult,
+            )
+
+        def column_factor(b, hf):
+            nc.vector.reciprocal(out=small["v2", b][:, hf : hf + 1], in_=small["col2", b][:, hf : hf + 1])
+
+        def gated(b, hf, a0, a1, number):
+            n = a1 - a0
+            pg = stage.tile([P, n * 512], BF16, name="pg", align_bytes=64)
+            cols = slice(512 * a0, 512 * a1)
+            nc.vector.scalar_tensor_tensor(
+                out=pg[:], in0=cost[b][hf][:, cols], scalar=small["v2", b][:, hf : hf + 1], in1=gate[b][:, cols],
+                op0=ALU.mult, op1=ALU.mult,
+            )
+            words = pg[:].bitcast(F32)
+            turned = bank("pg_turned", number)
+            for a in range(n):
+                for u in range(2):
+                    r = 2 * a + u
+                    nc.tensor.transpose(turned[:, r * P : (r + 1) * P], words[:, 256 * a + u : 256 * (a + 1) : 2], ident[:])
+            grouped = stage.tile([P, n * 512], BF16, name="pg_grouped", align_bytes=64)
+            nc.scalar.copy(
+                out=grouped[:].bitcast(F32).rearrange("p (a c u) -> p a c u", a=n, u=2),
+                in_=turned[:, 0 : n * 256].rearrange("p (a u c) -> p a c u", a=n, u=2),
+            )
+            held["pg", b, hf, a0] = grouped
+
+        def aggregate(b, hf, a0, a1, number):
+            n = a1 - a0
+            codes = stage.tile([P, n * P], U32, name="pg_codes", align_bytes=64)
+            scales = stage.tile([P, n * P], U8, name="pg_scales", align_bytes=64)
+            nc.vector.quantize_mx(out=codes[:].bitcast(FP8X4), scales=scales[:], in_=held["pg", b, hf, a0][:])
+            if a0 == 0:
+                held["v", b, hf] = bank("v_bank", number)
+            for a in range(a0, a1):
+                cols = slice((a - a0) * P, (a - a0 + 1) * P)
+                nc.tensor.matmul_mx(
+                    out=held["v", b, hf][:], lhsT=codes[:, cols].bitcast(FP8X4), lhsT_scale=scales[:, cols],
+                    rhs=f_codes[b][a][:].bitcast(FP8X4), rhs_scale=f_scales[b][a][:],
+                    start=(a == 0), stop=(a == PASSES - 1),
+                )
+
+        def root_mean_square(b, hf):
+            junk = stage.tile([P, E], BF16, name="junk_sq")
+            col = slice(hf, hf + 1)
+            nc.scalar.activation(out=junk[:], in_=held["v", b, hf][:], func=ACT.Square, accum_out=small["ss", b][:, col])
+            nc.scalar.activation(out=small["ms", b][:, col], in_=small["ss", b][:, col], func=ACT.Sqrt, scale=1.0 / E, bias=1e-6)
+
+        def norm_factor(b, hf):
+            nc.vector.reciprocal(out=small["rs", b][:, hf : hf + 1], in_=small["ms", b][:, hf : hf + 1])
+
+        def normalise(b, hf, engine):
+            y = stage.tile([P, E], F32, name="y")
+            rs = small["rs", b][:, hf : hf + 1]
+            if engine == "scalar":
+                nc.scalar.activation(out=y[:], in_=held["v", b, hf][:], func=ACT.Copy, scale=rs)
+            else:
+                nc.vector.tensor_scalar(out=y[:], in0=held["v", b, hf][:], scalar1=rs, scalar2=None, op0=ALU.mult)
+            nc.sync.dma_start(out=out[b, hf * P : (hf + 1) * P, :], in_=y[:])
+
+        steps = [(b, q) for b in both for q in range(GROUPS)]
+        last = len(steps) - 1
+        banks4 = [(k, hf) for k in range(2) for hf in range(HALVES)]
+
+        dustbin_scores()
+        nc.scalar.copy(out=hs[:, H : 2 * H], in_=hs[:, 0:H])
+        widen(0, 0, 2)
+        turn_h(0, 0)
+        for n in range(1, len(steps)):
+            group_h(*steps[n - 1])
+            if n >= 2:
+                scores(*steps[n - 2])
+            widen(*steps[n], 1)
+            turn_h(*steps[n])
+            if n == 1:
+                dustbin_column()
+            if n >= 2:
+                empty_scores(*steps[n - 2])
+            if n >= 3:
+                row_max(*steps[n - 3])
+                row_exp(*steps[n - 3])
+        group_h(*steps[last])
+        scores(*steps[last - 1])
+        empty_scores(*steps[last - 1])
+        row_max(*steps[last - 2])
+        row_exp(*steps[last - 2])
+        turn_scores(0, 0, 0)
+        turn_scores(0, 0, 1)
+        interleave_f(0, 0, "vector", 0, 2)
+        scores(*steps[last])
+        row_max(*steps[last - 1])
+        row_exp(*steps[last - 1])
+        turn_scores(0, 1, 0)
+        turn_scores(0, 1, 1)
+        turn_scores(1, 0, 0)
+        turn_scores(1, 0, 1)
+        interleave_f(0, 0, "vector", 1, 2)
+        empty_scores_and_max(*steps[last])
+        row_exp(*steps[last])
+        nc.scalar.activation(out=log_sum[:], in_=row_sum[:], func=ACT.Ln)
+        turn_scores(1, 1, 0)
+        turn_scores(1, 1, 1)
+        quantize_f(0, 0)
+        interleave_f(0, 1, "vector")
+        interleave_f(1, 0, "vector", 0, 2)
+        nc.vector.tensor_tensor(out=lse[:], in0=log_sum[:], in1=neg_max[:], op=ALU.subtract)
+        quantize_f(0, 1)
+        dust_partition_min()
+        add_lse(0, 0, 0)
+        add_lse(0, 0, 1)
+        add_lse(0, 1, 0)
+        column_min(0, 0, 0)
+        dust_partition_min2()
+        dust_spread(4)
+        add_lse(0, 1, 1)
+        column_min(0, 0, 1)
+        for k, hf in banks4:
+            add_lse(1, k, hf)
+        column_min(0, 1, 0)
+        column_exp(0, 0)
+        column_min(0, 1, 1)
+        dust_weights()
+        column_exp(0, 1)
+        column_min(1, 0, 0)
+        column_inverse(0, 0)
+        row_sums(0, 0, 6)
+        dust_total(4)
+        column_min(1, 0, 1)
+        column_min(1, 1, 0)
+        column_exp(1, 0)
+        column_inverse(0, 1)
+        row_sums(0, 1, 6)
+        column_min(1, 1, 1)
+        dust_mass()
+        column_exp(1, 1)
+        nc.scalar.activation(out=inv_root[:], in_=ones[:, 0:1], func=ACT.Sqrt, scale=1.0 / S)
+        interleave_f(1, 1, "scalar")
+        interleave_f(1, 0, "vector", 1, 2)
+        column_inverse(1, 0)
+        row_total(0)
+        row_inverse(0)
+        row_spread(0, (4, 5))
+        quantize_f(1, 0)
+        column_inverse(1, 1)
+        row_sums(1, 0, 7)
+        row_sums(1, 1, 7)
+        column_sum(0, 0, 0)
+        column_sum(0, 0, 1)
+        column_sum(0, 1, 0)
+        column_total(0, 0)
+        column_sum(0, 1, 1)
+        column_factor(0, 0)
+        row_total(1)
+        column_total(0, 1)
+        gated(0, 0, 0, 2, 2)
+        row_inverse(1)
+        row_spread(1, (0, 1))
+        column_factor(0, 1)
+        quantize_f(1, 1)
+        gated(0, 1, 0, 2, 3)
+        column_sum(1, 0, 0)
+        aggregate(0, 0, 0, 2, 4)
+        root_mean_square(0, 0)
+        column_sum(1, 0, 1)
+        column_sum(1, 1, 0)
+        column_total(1, 0)
+        aggregate(0, 1, 0, 2, 5)
+        root_mean_square(0, 1)
+        column_sum(1, 1, 1)
+        column_factor(1, 0)
+        norm_factor(0, 0)
+        normalise(0, 0, "scalar")
+        column_total(1, 1)
+        gated(1, 0, 0, 2, 6)
+        column_factor(1, 1)
+        norm_factor(0, 1)
+        gated(1, 1, 0, 1, 7)
+        normalise(0, 1, "scalar")
+        gated(1, 1, 1, 2, 0)
+        aggregate(1, 0, 0, 2, 2)
+        root_mean_square(1, 0)
+        aggregate(1, 1, 0, 1, 3)
+        aggregate(1, 1, 1, 2, 3)
+        root_mean_square(1, 1)
+        norm_factor(1, 0)
+        normalise(1, 0, "vector")
+        norm_factor(1, 1)
+        normalise(1, 1, "vector")

@@ -47,6 +47,7 @@ def tile_saladsinkhorndustbinaggregation_w8_kernel(tc, h_bytes, h_scale, wp_word
         inv_root = kept("inv_root", [P, 1], F32)
         z_rows = kept("z_rows", [P, P], BF16)
         neg_z_rows = kept("neg_z_rows", [P, P], F32)
+        hs_cols = kept("hs_cols", [P, 4], F32)
         hs = kept("hs", [P, 2 * H], F32)
         h_first = kept("hbytes_first", [P, 1, 2 * H], U8)
         h_rest = kept("hbytes_rest", [P, GROUPS - 1, 2 * H], U8)
@@ -78,7 +79,7 @@ def tile_saladsinkhorndustbinaggregation_w8_kernel(tc, h_bytes, h_scale, wp_word
                 small[name, b] = kept("%s_%d" % (name, b), [P, width], F32)
 
         nc.scalar.dma_start(out=z_rows[0 : B * TILES, :], in_=z.rearrange("b (j m) -> (b j) m", m=P))
-        nc.sync.dma_start(out=hs[:, 0:H], in_=h_scale.rearrange("a o k -> (a o k)").partition_broadcast(P))
+        nc.sync.dma_start(out=hs_cols[:], in_=h_scale.rearrange("a o (p t) -> p (a o t)", t=4))
 
         def load_h(dst, b, q0, q1):
             rows = h_bytes[b, 256 * q0 : 256 * q1, :]
@@ -88,10 +89,10 @@ def tile_saladsinkhorndustbinaggregation_w8_kernel(tc, h_bytes, h_scale, wp_word
             rows = f[b, 512 * a : 512 * (a + 1), :]
             nc.sync.dma_start(out=f_raw[b][a][:], in_=rows.rearrange("(p t) e -> p t e", t=4))
 
-        nc.gpsimd.memset(w_scales[:].bitcast(I32), 0)
         make_identity(nc, ident[:])
-        nc.gpsimd.memset(neg_z_rows[:], 0.0)
+        nc.gpsimd.memset(w_scales[:].bitcast(I32), 0)
         nc.gpsimd.memset(ones[:], 1.0)
+        nc.gpsimd.memset(neg_z_rows[:], 0.0)
 
         load_h(h_first, 0, 0, 1)
         load_h(h_rest, 0, 1, GROUPS)
@@ -113,12 +114,37 @@ def tile_saladsinkhorndustbinaggregation_w8_kernel(tc, h_bytes, h_scale, wp_word
         held = {}
         def dustbin_scores():
             nc.scalar.activation(out=neg_z_rows[0 : B * TILES, :], in_=z_rows[0 : B * TILES, :], func=ACT.Copy, scale=-1.0)
+
+        def dustbin_turn():
             z_bank = bank("z_bank", 4)
             nc.tensor.transpose(z_bank[:, 0:P], neg_z_rows[:], ident[:])
             held["z"] = z_bank
 
+        def spread_scales():
+            sb = bank("scale_bank", 5)
+            for t in range(4):
+                nc.tensor.transpose(sb[:, t * P : (t + 1) * P], hs_cols[:, t : t + 1].to_broadcast([P, P]), ident[:])
+            nc.vector.tensor_copy(out=hs[:, 0:H].rearrange("p (n t) -> p n t", t=4), in_=sb[:].rearrange("p (t n) -> p n t", t=4))
+            nc.scalar.copy(out=hs[:, H : 2 * H], in_=hs[:, 0:H])
+
         def dustbin_column():
             nc.vector.tensor_copy(out=neg_all[:, :, C], in_=held["z"][:, 0 : B * TILES])
+
+        scratch = bank("scratch", 7)
+
+        def warm_plain(count):
+            for i in range(count):
+                nc.tensor.matmul(out=scratch[:, 0:P], lhsT=ones[:], rhs=ident[:], start=True, stop=True)
+
+        def warm_after(column):
+            nc.tensor.matmul(out=scratch[:, 0:C], lhsT=ones[:], rhs=column.to_broadcast([P, C]), start=True, stop=True)
+
+        def warm(count, codes=w_codes, scales=w_scales):
+            for i in range(count):
+                nc.tensor.matmul_mx(
+                    out=scratch[:, 0:C], lhsT=w_codes[:, 0:P].bitcast(FP8X4), lhsT_scale=w_scales[:, 0:P],
+                    rhs=codes[:, 0:C].bitcast(FP8X4), rhs_scale=scales[:, 0:C], start=True, stop=True,
+                )
 
 
         def widen(b, q, pieces):
@@ -214,7 +240,7 @@ def tile_saladsinkhorndustbinaggregation_w8_kernel(tc, h_bytes, h_scale, wp_word
             )
 
         def cost_bank_number(b, k, hf):
-            return (4 + 4 * b + 2 * k + hf) % 8
+            return (4, 5, 6, 0, 1, 2, 3, 4)[4 * b + 2 * k + hf]
 
         def turn_scores(b, k, hf):
             nb = bank("cost_bank", cost_bank_number(b, k, hf))
@@ -231,7 +257,7 @@ def tile_saladsinkhorndustbinaggregation_w8_kernel(tc, h_bytes, h_scale, wp_word
                 n = b * TILES + 4 * k + jj
                 nc.tensor.matmul(
                     out=nb[:, jj * P : (jj + 1) * P], lhsT=lse[:, n : n + 1].to_broadcast([P, P]), rhs=ident[:],
-                    is_transpose=True, start=False, stop=(jj == 3),
+                    is_transpose=(jj > 0), start=False, stop=(jj == 3),
                 )
 
         def column_min(b, k, hf):
@@ -287,10 +313,10 @@ def tile_saladsinkhorndustbinaggregation_w8_kernel(tc, h_bytes, h_scale, wp_word
         def column_inverse(b, hf):
             nc.vector.reciprocal(out=small["v1", b][:, hf : hf + 1], in_=small["col1", b][:, hf : hf + 1])
 
-        def row_sums(b, hf, number):
-            if hf == 0:
+        def row_sums(b, hf, number, j0=0, j1=TILES):
+            if hf == 0 and j0 == 0:
                 held["rows", b] = bank("row_bank", number)
-            for j in range(TILES):
+            for j in range(j0, j1):
                 nc.tensor.matmul(
                     out=held["rows", b][:, j * SUM_N : (j + 1) * SUM_N], lhsT=cost[b][hf][:, j * P : (j + 1) * P],
                     rhs=small["v1", b][:, hf : hf + 1].to_broadcast([P, SUM_N]),
@@ -388,13 +414,17 @@ def tile_saladsinkhorndustbinaggregation_w8_kernel(tc, h_bytes, h_scale, wp_word
         banks4 = [(k, hf) for k in range(2) for hf in range(HALVES)]
 
         dustbin_scores()
-        nc.scalar.copy(out=hs[:, H : 2 * H], in_=hs[:, 0:H])
+        spread_scales()
+        dustbin_turn()
+        warm_plain(3)
         widen(0, 0, 2)
         turn_h(0, 0)
+        warm(4)
         for n in range(1, len(steps)):
             group_h(*steps[n - 1])
             if n >= 2:
                 scores(*steps[n - 2])
+            warm(3 if n >= 2 else 4)
             widen(*steps[n], 1)
             turn_h(*steps[n])
             if n == 1:
@@ -406,6 +436,7 @@ def tile_saladsinkhorndustbinaggregation_w8_kernel(tc, h_bytes, h_scale, wp_word
                 row_exp(*steps[n - 3])
         group_h(*steps[last])
         scores(*steps[last - 1])
+        warm(3)
         empty_scores(*steps[last - 1])
         row_max(*steps[last - 2])
         row_exp(*steps[last - 2])
@@ -413,19 +444,22 @@ def tile_saladsinkhorndustbinaggregation_w8_kernel(tc, h_bytes, h_scale, wp_word
         turn_scores(0, 0, 1)
         interleave_f(0, 0, "vector", 0, 2)
         scores(*steps[last])
+        warm(3)
         row_max(*steps[last - 1])
         row_exp(*steps[last - 1])
         turn_scores(0, 1, 0)
         turn_scores(0, 1, 1)
         turn_scores(1, 0, 0)
         turn_scores(1, 0, 1)
+        warm(4)
         interleave_f(0, 0, "vector", 1, 2)
         empty_scores_and_max(*steps[last])
         row_exp(*steps[last])
         nc.scalar.activation(out=log_sum[:], in_=row_sum[:], func=ACT.Ln)
+        interleave_f(1, 1, "scalar", 0, 2)
         turn_scores(1, 1, 0)
-        turn_scores(1, 1, 1)
         quantize_f(0, 0)
+        warm(4, f_codes[0][0], f_scales[0][0])
         interleave_f(0, 1, "vector")
         interleave_f(1, 0, "vector", 0, 2)
         nc.vector.tensor_tensor(out=lse[:], in0=log_sum[:], in1=neg_max[:], op=ALU.subtract)
@@ -436,11 +470,14 @@ def tile_saladsinkhorndustbinaggregation_w8_kernel(tc, h_bytes, h_scale, wp_word
         add_lse(0, 1, 0)
         column_min(0, 0, 0)
         dust_partition_min2()
-        dust_spread(4)
         add_lse(0, 1, 1)
         column_min(0, 0, 1)
-        for k, hf in banks4:
-            add_lse(1, k, hf)
+        dust_spread(5)
+        add_lse(1, 0, 0)
+        add_lse(1, 0, 1)
+        add_lse(1, 1, 0)
+        turn_scores(1, 1, 1)
+        add_lse(1, 1, 1)
         column_min(0, 1, 0)
         column_exp(0, 0)
         column_min(0, 1, 1)
@@ -448,64 +485,68 @@ def tile_saladsinkhorndustbinaggregation_w8_kernel(tc, h_bytes, h_scale, wp_word
         column_exp(0, 1)
         column_min(1, 0, 0)
         column_inverse(0, 0)
+        dust_total(5)
         row_sums(0, 0, 6)
-        dust_total(4)
         column_min(1, 0, 1)
+        dust_mass()
         column_min(1, 1, 0)
         column_exp(1, 0)
         column_inverse(0, 1)
         row_sums(0, 1, 6)
         column_min(1, 1, 1)
-        dust_mass()
         column_exp(1, 1)
         nc.scalar.activation(out=inv_root[:], in_=ones[:, 0:1], func=ACT.Sqrt, scale=1.0 / S)
-        interleave_f(1, 1, "scalar")
+        interleave_f(1, 1, "scalar", 1, 2)
         interleave_f(1, 0, "vector", 1, 2)
         column_inverse(1, 0)
+        row_sums(1, 0, 4, 0, 3)
         row_total(0)
         row_inverse(0)
-        row_spread(0, (4, 5))
+        row_spread(0, (0, 5))
         quantize_f(1, 0)
         column_inverse(1, 1)
-        row_sums(1, 0, 7)
-        row_sums(1, 1, 7)
+        row_sums(1, 0, 4, 3, TILES)
+        row_sums(1, 1, 4)
+        warm(4)
         column_sum(0, 0, 0)
         column_sum(0, 0, 1)
         column_sum(0, 1, 0)
         column_total(0, 0)
         column_sum(0, 1, 1)
         column_factor(0, 0)
-        row_total(1)
-        column_total(0, 1)
-        gated(0, 0, 0, 2, 2)
-        row_inverse(1)
-        row_spread(1, (0, 1))
-        column_factor(0, 1)
         quantize_f(1, 1)
-        gated(0, 1, 0, 2, 3)
+        warm(4, f_codes[1][1], f_scales[1][1])
+        column_total(0, 1)
+        gated(0, 0, 0, 2, 3)
+        row_total(1)
+        column_factor(0, 1)
+        row_inverse(1)
+        row_spread(1, (1, 2))
+        gated(0, 1, 0, 2, 6)
         column_sum(1, 0, 0)
         aggregate(0, 0, 0, 2, 4)
         root_mean_square(0, 0)
         column_sum(1, 0, 1)
         column_sum(1, 1, 0)
         column_total(1, 0)
-        aggregate(0, 1, 0, 2, 5)
-        root_mean_square(0, 1)
         column_sum(1, 1, 1)
         column_factor(1, 0)
+        aggregate(0, 1, 0, 2, 0)
+        column_total(1, 1)
         norm_factor(0, 0)
         normalise(0, 0, "scalar")
-        column_total(1, 1)
-        gated(1, 0, 0, 2, 6)
+        root_mean_square(0, 1)
+        warm_after(small["col2", 1][:, 1:2])
+        gated(1, 0, 0, 2, 5)
         column_factor(1, 1)
+        gated(1, 1, 0, 1, 3)
+        gated(1, 1, 1, 2, 6)
+        aggregate(1, 0, 0, 2, 1)
         norm_factor(0, 1)
-        gated(1, 1, 0, 1, 7)
-        normalise(0, 1, "scalar")
-        gated(1, 1, 1, 2, 0)
-        aggregate(1, 0, 0, 2, 2)
+        aggregate(1, 1, 0, 1, 2)
+        aggregate(1, 1, 1, 2, 2)
         root_mean_square(1, 0)
-        aggregate(1, 1, 0, 1, 3)
-        aggregate(1, 1, 1, 2, 3)
+        normalise(0, 1, "vector")
         root_mean_square(1, 1)
         norm_factor(1, 0)
         normalise(1, 0, "vector")

@@ -1,3 +1,4 @@
+import math
 from contextlib import ExitStack
 
 import concourse.mybir as mybir
@@ -23,7 +24,7 @@ TILES = S // P
 GROUPS = S // 256
 HALVES = C // P
 PASSES = S // 512
-SUM_N = 48
+SUM_N = 64
 ROW = 264
 
 
@@ -66,6 +67,7 @@ def tile_saladsinkhorndustbinaggregation_w8_kernel(tc, h_bytes, h_scale, wp_word
         dust_min_p = kept("dust_min_p", [P, B], F32)
         dust_min = kept("dust_min", [P, B], F32)
         dust_sum_p = kept("dust_sum_p", [P, B], F32)
+        upper_sum = kept("upper_sum", [P, 4], F32)
         dust_inv = kept("dust_inv", [P, B], F32)
         neg_max = kept("neg_max", [P, B * TILES], F32)
         row_sum = kept("row_sum", [P, B * TILES], F32)
@@ -78,7 +80,6 @@ def tile_saladsinkhorndustbinaggregation_w8_kernel(tc, h_bytes, h_scale, wp_word
                                 ("v2", 2), ("ss", 2), ("ms", 2), ("rs", 2)):
                 small[name, b] = kept("%s_%d" % (name, b), [P, width], F32)
 
-        nc.scalar.dma_start(out=z_rows[0 : B * TILES, :], in_=z.rearrange("b (j m) -> (b j) m", m=P))
         nc.sync.dma_start(out=hs_cols[:], in_=h_scale.rearrange("a o (p t) -> p (a o t)", t=4))
 
         def load_h(dst, b, q0, q1):
@@ -89,8 +90,8 @@ def tile_saladsinkhorndustbinaggregation_w8_kernel(tc, h_bytes, h_scale, wp_word
             rows = f[b, 512 * a : 512 * (a + 1), :]
             nc.sync.dma_start(out=f_raw[b][a][:], in_=rows.rearrange("(p t) e -> p t e", t=4))
 
-        make_identity(nc, ident[:])
         nc.gpsimd.memset(w_scales[:].bitcast(I32), 0)
+        make_identity(nc, ident[:])
         nc.gpsimd.memset(ones[:], 1.0)
         nc.gpsimd.memset(neg_z_rows[:], 0.0)
 
@@ -99,15 +100,17 @@ def tile_saladsinkhorndustbinaggregation_w8_kernel(tc, h_bytes, h_scale, wp_word
         nc.sync.dma_start(
             out=w_codes[:].bitcast(I32), in_=wp_words[0].rearrange("p n t -> p (n t)").bitcast(I32)
         )
+        load_f(0, 0)
         for quad in range(4):
             nc.sync.dma_start(
                 out=w_scales[32 * quad : 32 * quad + 4, :].bitcast(I32),
                 in_=wp_scales[0, 4 * quad : 4 * quad + 4, :].bitcast(I32),
             )
+        nc.sync.dma_start(out=z_rows[0 : B * TILES, :], in_=z.rearrange("b (j m) -> (b j) m", m=P))
         load_h(h_second, 1, 0, GROUPS)
-        for b in both:
-            for a in range(PASSES):
-                load_f(b, a)
+        load_f(0, 1)
+        load_f(1, 0)
+        load_f(1, 1)
         for b in both:
             nc.sync.dma_start(out=gate[b][:], in_=g[b].partition_broadcast(P))
 
@@ -135,9 +138,6 @@ def tile_saladsinkhorndustbinaggregation_w8_kernel(tc, h_bytes, h_scale, wp_word
         def warm_plain(count):
             for i in range(count):
                 nc.tensor.matmul(out=scratch[:, 0:P], lhsT=ones[:], rhs=ident[:], start=True, stop=True)
-
-        def warm_after(column):
-            nc.tensor.matmul(out=scratch[:, 0:C], lhsT=ones[:], rhs=column.to_broadcast([P, C]), start=True, stop=True)
 
         def warm(count, codes=w_codes, scales=w_scales):
             for i in range(count):
@@ -240,7 +240,7 @@ def tile_saladsinkhorndustbinaggregation_w8_kernel(tc, h_bytes, h_scale, wp_word
             )
 
         def cost_bank_number(b, k, hf):
-            return (4, 5, 6, 0, 1, 2, 3, 4)[4 * b + 2 * k + hf]
+            return (4, 5, 6, 0, 1, 2, 3, 6)[4 * b + 2 * k + hf]
 
         def turn_scores(b, k, hf):
             nb = bank("cost_bank", cost_bank_number(b, k, hf))
@@ -257,7 +257,7 @@ def tile_saladsinkhorndustbinaggregation_w8_kernel(tc, h_bytes, h_scale, wp_word
                 n = b * TILES + 4 * k + jj
                 nc.tensor.matmul(
                     out=nb[:, jj * P : (jj + 1) * P], lhsT=lse[:, n : n + 1].to_broadcast([P, P]), rhs=ident[:],
-                    is_transpose=(jj > 0), start=False, stop=(jj == 3),
+                    is_transpose=(jj > 0 or (k, hf) == (0, 0)), start=False, stop=(jj == 3),
                 )
 
         def column_min(b, k, hf):
@@ -280,10 +280,12 @@ def tile_saladsinkhorndustbinaggregation_w8_kernel(tc, h_bytes, h_scale, wp_word
                 nc.tensor.transpose(db[:, b * P : (b + 1) * P], dust_min_p[:, b : b + 1].to_broadcast([P, P]), ident[:])
             held["dust"] = db
 
-        def dust_weights():
+        def dust_weights_min():
             nc.vector.tensor_reduce(
                 out=dust_min[:], in_=held["dust"][:, 0 : B * P].rearrange("p (b m) -> p b m", b=B), axis=AX.X, op=ALU.min
             )
+
+        def dust_weights():
             for b in both:
                 cols = slice(b * TILES, (b + 1) * TILES)
                 nc.scalar.activation(
@@ -313,18 +315,42 @@ def tile_saladsinkhorndustbinaggregation_w8_kernel(tc, h_bytes, h_scale, wp_word
         def column_inverse(b, hf):
             nc.vector.reciprocal(out=small["v1", b][:, hf : hf + 1], in_=small["col1", b][:, hf : hf + 1])
 
-        def row_sums(b, hf, number, j0=0, j1=TILES):
+        def row_sums(b, hf, number, j0, j1, tiles):
             if hf == 0 and j0 == 0:
                 held["rows", b] = bank("row_bank", number)
             for j in range(j0, j1):
                 nc.tensor.matmul(
                     out=held["rows", b][:, j * SUM_N : (j + 1) * SUM_N], lhsT=cost[b][hf][:, j * P : (j + 1) * P],
                     rhs=small["v1", b][:, hf : hf + 1].to_broadcast([P, SUM_N]),
-                    start=(hf == 0 and j == 0), stop=(hf == HALVES - 1 and j == TILES - 1),
+                    start=(hf == 0 and j == 0), stop=(hf == HALVES - 1 and j == tiles - 1),
                 )
 
-        def row_total(b):
-            nc.vector.tensor_tensor(out=small["row2", b][:], in0=held["rows", b][:, 0 : TILES * SUM_N : SUM_N], in1=small["dust", b][:], op=ALU.add)
+        def row_total(b, tiles):
+            nc.vector.tensor_tensor(
+                out=small["row2", b][:, 0:tiles], in0=held["rows", b][:, 0 : tiles * SUM_N : SUM_N],
+                in1=small["dust", b][:, 0:tiles], op=ALU.add,
+            )
+
+        def scale_upper(hf):
+            upper = cost[0][hf][:, BANK:S]
+            nc.vector.tensor_scalar(out=upper, in0=upper, scalar1=small["v1", 0][:, hf : hf + 1], scalar2=None, op0=ALU.mult)
+
+        def turn_upper(hf, number):
+            if hf == 0:
+                held["upper"] = bank("upper_bank", number)
+            for jj in range(4):
+                nc.tensor.matmul(
+                    out=held["upper"][:, jj * P : (jj + 1) * P], lhsT=cost[0][hf][:, BANK + jj * P : BANK + (jj + 1) * P],
+                    rhs=ident[:], is_transpose=True, start=(hf == 0 and jj == 0), stop=(hf == HALVES - 1 and jj == 3),
+                )
+
+        def sum_upper():
+            nc.vector.tensor_reduce(
+                out=upper_sum[:], in_=held["upper"][:].rearrange("p (j c) -> p j c", j=4), axis=AX.X, op=ALU.add
+            )
+
+        def total_upper():
+            nc.vector.tensor_tensor(out=small["row2", 0][:, 4:TILES], in0=upper_sum[:], in1=small["dust", 0][:, 4:TILES], op=ALU.add)
 
         def row_inverse(b):
             nc.vector.reciprocal(out=small["u2", b][:], in_=small["row2", b][:])
@@ -340,8 +366,8 @@ def tile_saladsinkhorndustbinaggregation_w8_kernel(tc, h_bytes, h_scale, wp_word
         def column_sum(b, hf, k):
             cols = slice(k * BANK, (k + 1) * BANK)
             nc.vector.scalar_tensor_tensor(
-                out=cost[b][hf][:, cols], in0=cost[b][hf][:, cols], scalar=small["v1", b][:, hf : hf + 1],
-                in1=held["u", b, k][:], op0=ALU.mult, op1=ALU.mult,
+                out=cost[b][hf][:, cols], in0=cost[b][hf][:, cols],
+                scalar=(1.0 if (b, k) == (0, 1) else small["v1", b][:, hf : hf + 1]), in1=held["u", b, k][:], op0=ALU.mult, op1=ALU.mult,
                 accum_out=small["col2p", b][:, 2 * hf + k : 2 * hf + k + 1],
             )
 
@@ -349,7 +375,7 @@ def tile_saladsinkhorndustbinaggregation_w8_kernel(tc, h_bytes, h_scale, wp_word
             c2 = small["col2p", b]
             nc.vector.tensor_scalar(
                 out=small["col2", b][:, hf : hf + 1], in0=c2[:, 2 * hf : 2 * hf + 1], scalar1=c2[:, 2 * hf + 1 : 2 * hf + 2],
-                scalar2=inv_root[:], op0=ALU.add, op1=ALU.mult,
+                scalar2=1.0 / math.sqrt(S), op0=ALU.add, op1=ALU.mult,
             )
 
         def column_factor(b, hf):
@@ -369,8 +395,13 @@ def tile_saladsinkhorndustbinaggregation_w8_kernel(tc, h_bytes, h_scale, wp_word
                 for u in range(2):
                     r = 2 * a + u
                     nc.tensor.transpose(turned[:, r * P : (r + 1) * P], words[:, 256 * a + u : 256 * (a + 1) : 2], ident[:])
+            held["pg_turned", b, hf, a0] = turned
+
+        def group_pg(b, hf, a0, a1, copy=nc.scalar.copy):
+            n = a1 - a0
+            turned = held["pg_turned", b, hf, a0]
             grouped = stage.tile([P, n * 512], BF16, name="pg_grouped", align_bytes=64)
-            nc.scalar.copy(
+            copy(
                 out=grouped[:].bitcast(F32).rearrange("p (a c u) -> p a c u", a=n, u=2),
                 in_=turned[:, 0 : n * 256].rearrange("p (a u c) -> p a c u", a=n, u=2),
             )
@@ -391,43 +422,55 @@ def tile_saladsinkhorndustbinaggregation_w8_kernel(tc, h_bytes, h_scale, wp_word
                     start=(a == 0), stop=(a == PASSES - 1),
                 )
 
-        def root_mean_square(b, hf):
+        def square_sum(b, hf):
             junk = stage.tile([P, E], BF16, name="junk_sq")
             col = slice(hf, hf + 1)
-            nc.scalar.activation(out=junk[:], in_=held["v", b, hf][:], func=ACT.Square, accum_out=small["ss", b][:, col])
-            nc.scalar.activation(out=small["ms", b][:, col], in_=small["ss", b][:, col], func=ACT.Sqrt, scale=1.0 / E, bias=1e-6)
+            nc.scalar.activation(out=junk[:], in_=held["v", b, hf][:], func=ACT.Square, scale=inv_root[:], accum_out=small["ss", b][:, col])
+
+        def root(b, hf):
+            col = slice(hf, hf + 1)
+            nc.scalar.activation(out=small["ms", b][:, col], in_=small["ss", b][:, col], func=ACT.Sqrt, bias=1e-6)
 
         def norm_factor(b, hf):
             nc.vector.reciprocal(out=small["rs", b][:, hf : hf + 1], in_=small["ms", b][:, hf : hf + 1])
 
-        def normalise(b, hf, engine):
-            y = stage.tile([P, E], F32, name="y")
+        def normalise(b, hf, engine, part=0, parts=1):
+            cols = slice(part * E // parts, (part + 1) * E // parts)
+            y = kept("y_%d_%d_%d" % (b, hf, part), [P, E // parts], F32)
             rs = small["rs", b][:, hf : hf + 1]
             if engine == "scalar":
-                nc.scalar.activation(out=y[:], in_=held["v", b, hf][:], func=ACT.Copy, scale=rs)
+                nc.scalar.activation(out=y[:], in_=held["v", b, hf][:, cols], func=ACT.Copy, scale=rs)
             else:
-                nc.vector.tensor_scalar(out=y[:], in0=held["v", b, hf][:], scalar1=rs, scalar2=None, op0=ALU.mult)
-            nc.sync.dma_start(out=out[b, hf * P : (hf + 1) * P, :], in_=y[:])
+                nc.vector.tensor_scalar(out=y[:], in0=held["v", b, hf][:, cols], scalar1=rs, scalar2=None, op0=ALU.mult)
+            nc.sync.dma_start(out=out[b, hf * P : (hf + 1) * P, cols], in_=y[:])
 
         steps = [(b, q) for b in both for q in range(GROUPS)]
         last = len(steps) - 1
         banks4 = [(k, hf) for k in range(2) for hf in range(HALVES)]
 
-        dustbin_scores()
         spread_scales()
-        dustbin_turn()
         warm_plain(3)
         widen(0, 0, 2)
         turn_h(0, 0)
+        interleave_f(0, 0, "scalar", 0, 4)
         warm(4)
         for n in range(1, len(steps)):
             group_h(*steps[n - 1])
+            if n == 1:
+                dustbin_scores()
+                interleave_f(0, 0, "scalar", 1, 4)
+                interleave_f(0, 0, "scalar", 2, 4)
+            if n == 3:
+                quantize_f(0, 0)
             if n >= 2:
                 scores(*steps[n - 2])
-            warm(3 if n >= 2 else 4)
+            warm(3 if n >= 2 else 1)
             widen(*steps[n], 1)
             turn_h(*steps[n])
             if n == 1:
+                dustbin_turn()
+                interleave_f(0, 0, "vector", 3, 4)
+            if n == 2:
                 dustbin_column()
             if n >= 2:
                 empty_scores(*steps[n - 2])
@@ -442,7 +485,7 @@ def tile_saladsinkhorndustbinaggregation_w8_kernel(tc, h_bytes, h_scale, wp_word
         row_exp(*steps[last - 2])
         turn_scores(0, 0, 0)
         turn_scores(0, 0, 1)
-        interleave_f(0, 0, "vector", 0, 2)
+        interleave_f(0, 1, "vector", 0, 2)
         scores(*steps[last])
         warm(3)
         row_max(*steps[last - 1])
@@ -452,61 +495,68 @@ def tile_saladsinkhorndustbinaggregation_w8_kernel(tc, h_bytes, h_scale, wp_word
         turn_scores(1, 0, 0)
         turn_scores(1, 0, 1)
         warm(4)
-        interleave_f(0, 0, "vector", 1, 2)
+        interleave_f(0, 1, "vector", 2, 4)
         empty_scores_and_max(*steps[last])
         row_exp(*steps[last])
         nc.scalar.activation(out=log_sum[:], in_=row_sum[:], func=ACT.Ln)
         interleave_f(1, 1, "scalar", 0, 2)
         turn_scores(1, 1, 0)
-        quantize_f(0, 0)
-        warm(4, f_codes[0][0], f_scales[0][0])
-        interleave_f(0, 1, "vector")
+        interleave_f(0, 1, "vector", 3, 4)
         interleave_f(1, 0, "vector", 0, 2)
-        nc.vector.tensor_tensor(out=lse[:], in0=log_sum[:], in1=neg_max[:], op=ALU.subtract)
         quantize_f(0, 1)
+        warm(4, f_codes[0][1], f_scales[0][1])
+        interleave_f(1, 0, "vector", 1, 2)
+        nc.vector.tensor_tensor(out=lse[:], in0=log_sum[:], in1=neg_max[:], op=ALU.subtract)
+        interleave_f(1, 1, "vector", 1, 2)
         dust_partition_min()
         add_lse(0, 0, 0)
-        add_lse(0, 0, 1)
         add_lse(0, 1, 0)
+        add_lse(0, 0, 1)
         column_min(0, 0, 0)
         dust_partition_min2()
         add_lse(0, 1, 1)
-        column_min(0, 0, 1)
-        dust_spread(5)
-        add_lse(1, 0, 0)
-        add_lse(1, 0, 1)
-        add_lse(1, 1, 0)
-        turn_scores(1, 1, 1)
-        add_lse(1, 1, 1)
+        dust_spread(4)
         column_min(0, 1, 0)
         column_exp(0, 0)
+        add_lse(1, 0, 0)
+        add_lse(1, 1, 0)
+        add_lse(1, 0, 1)
+        turn_scores(1, 1, 1)
+        add_lse(1, 1, 1)
+        column_min(0, 0, 1)
+        dust_weights_min()
         column_min(0, 1, 1)
-        dust_weights()
         column_exp(0, 1)
-        column_min(1, 0, 0)
+        dust_weights()
         column_inverse(0, 0)
-        dust_total(5)
-        row_sums(0, 0, 6)
-        column_min(1, 0, 1)
-        dust_mass()
+        row_sums(0, 0, 5, 0, 4, 4)
+        column_min(1, 0, 0)
+        scale_upper(0)
+        turn_upper(0, 0)
         column_min(1, 1, 0)
         column_exp(1, 0)
         column_inverse(0, 1)
-        row_sums(0, 1, 6)
+        dust_total(4)
+        row_sums(0, 1, 5, 0, 2, 4)
+        scale_upper(1)
+        turn_upper(1, 0)
+        row_sums(0, 1, 5, 2, 4, 4)
+        column_min(1, 0, 1)
+        dust_mass()
         column_min(1, 1, 1)
         column_exp(1, 1)
-        nc.scalar.activation(out=inv_root[:], in_=ones[:, 0:1], func=ACT.Sqrt, scale=1.0 / S)
-        interleave_f(1, 1, "scalar", 1, 2)
-        interleave_f(1, 0, "vector", 1, 2)
         column_inverse(1, 0)
-        row_sums(1, 0, 4, 0, 3)
-        row_total(0)
+        row_sums(1, 0, 4, 0, 4, TILES)
+        sum_upper()
+        row_total(0, 4)
+        total_upper()
         row_inverse(0)
         row_spread(0, (0, 5))
+        row_sums(1, 0, 4, 4, TILES, TILES)
+        nc.scalar.activation(out=inv_root[:], in_=ones[:, 0:1], func=ACT.Sqrt, scale=1.0 / E)
         quantize_f(1, 0)
         column_inverse(1, 1)
-        row_sums(1, 0, 4, 3, TILES)
-        row_sums(1, 1, 4)
+        row_sums(1, 1, 4, 0, TILES, TILES)
         warm(4)
         column_sum(0, 0, 0)
         column_sum(0, 0, 1)
@@ -514,41 +564,52 @@ def tile_saladsinkhorndustbinaggregation_w8_kernel(tc, h_bytes, h_scale, wp_word
         column_total(0, 0)
         column_sum(0, 1, 1)
         column_factor(0, 0)
-        quantize_f(1, 1)
-        warm(4, f_codes[1][1], f_scales[1][1])
         column_total(0, 1)
         gated(0, 0, 0, 2, 3)
-        row_total(1)
         column_factor(0, 1)
+        row_total(1, TILES)
         row_inverse(1)
         row_spread(1, (1, 2))
+        warm(4)
+        group_pg(0, 0, 0, 2)
         gated(0, 1, 0, 2, 6)
+        group_pg(0, 1, 0, 2)
         column_sum(1, 0, 0)
         aggregate(0, 0, 0, 2, 4)
-        root_mean_square(0, 0)
+        square_sum(0, 0)
+        root(0, 0)
         column_sum(1, 0, 1)
         column_sum(1, 1, 0)
         column_total(1, 0)
         column_sum(1, 1, 1)
         column_factor(1, 0)
-        aggregate(0, 1, 0, 2, 0)
         column_total(1, 1)
-        norm_factor(0, 0)
-        normalise(0, 0, "scalar")
-        root_mean_square(0, 1)
-        warm_after(small["col2", 1][:, 1:2])
-        gated(1, 0, 0, 2, 5)
+        aggregate(0, 1, 0, 2, 0)
+        warm(4)
         column_factor(1, 1)
+        square_sum(0, 1)
+        root(0, 1)
+        gated(1, 0, 0, 2, 5)
+        group_pg(1, 0, 0, 2)
         gated(1, 1, 0, 1, 3)
         gated(1, 1, 1, 2, 6)
-        aggregate(1, 0, 0, 2, 1)
+        warm(4)
+        norm_factor(0, 0)
         norm_factor(0, 1)
+        normalise(0, 0, "scalar")
+        normalise(0, 1, "scalar")
+        quantize_f(1, 1)
+        aggregate(1, 0, 0, 2, 1)
+        group_pg(1, 1, 0, 1, nc.vector.tensor_copy)
+        group_pg(1, 1, 1, 2, nc.vector.tensor_copy)
         aggregate(1, 1, 0, 1, 2)
         aggregate(1, 1, 1, 2, 2)
-        root_mean_square(1, 0)
-        normalise(0, 1, "vector")
-        root_mean_square(1, 1)
+        square_sum(1, 0)
+        root(1, 0)
+        square_sum(1, 1)
+        root(1, 1)
         norm_factor(1, 0)
         normalise(1, 0, "vector")
         norm_factor(1, 1)
-        normalise(1, 1, "vector")
+        normalise(1, 1, "vector", 0, 2)
+        normalise(1, 1, "vector", 1, 2)

@@ -139,6 +139,9 @@ def tile_saladsinkhorndustbinaggregation_w8_kernel(tc, h_bytes, h_scale, wp_word
             for i in range(count):
                 nc.tensor.matmul(out=scratch[:, 0:P], lhsT=ones[:], rhs=ident[:], start=True, stop=True)
 
+        def warm_after(column):
+            nc.tensor.matmul(out=scratch[:, 0:C], lhsT=ones[:], rhs=column.to_broadcast([P, C]), start=True, stop=True)
+
         def warm(count, codes=w_codes, scales=w_scales):
             for i in range(count):
                 nc.tensor.matmul_mx(
@@ -352,8 +355,8 @@ def tile_saladsinkhorndustbinaggregation_w8_kernel(tc, h_bytes, h_scale, wp_word
         def total_upper():
             nc.vector.tensor_tensor(out=small["row2", 0][:, 4:TILES], in0=upper_sum[:], in1=small["dust", 0][:, 4:TILES], op=ALU.add)
 
-        def row_inverse(b):
-            nc.vector.reciprocal(out=small["u2", b][:], in_=small["row2", b][:])
+        def row_inverse(b, j0=0, j1=TILES):
+            nc.vector.reciprocal(out=small["u2", b][:, j0:j1], in_=small["row2", b][:, j0:j1])
 
         def row_spread(b, numbers):
             for k in range(2):
@@ -372,10 +375,10 @@ def tile_saladsinkhorndustbinaggregation_w8_kernel(tc, h_bytes, h_scale, wp_word
             )
 
         def column_total(b, hf):
-            c2 = small["col2p", b]
-            nc.vector.tensor_scalar(
-                out=small["col2", b][:, hf : hf + 1], in0=c2[:, 2 * hf : 2 * hf + 1], scalar1=c2[:, 2 * hf + 1 : 2 * hf + 2],
-                scalar2=1.0 / math.sqrt(S), op0=ALU.add, op1=ALU.mult,
+            halves = stage.tile([P, 2], F32, name="junk_total")
+            nc.scalar.activation(
+                out=halves[:], in_=small["col2p", b][:, 2 * hf : 2 * hf + 2], func=ACT.Copy, scale=1.0 / math.sqrt(S),
+                accum_out=small["col2", b][:, hf : hf + 1],
             )
 
         def column_factor(b, hf):
@@ -449,65 +452,66 @@ def tile_saladsinkhorndustbinaggregation_w8_kernel(tc, h_bytes, h_scale, wp_word
         banks4 = [(k, hf) for k in range(2) for hf in range(HALVES)]
 
         spread_scales()
-        warm_plain(3)
+        warm_plain(4)
         widen(0, 0, 2)
         turn_h(0, 0)
         interleave_f(0, 0, "scalar", 0, 4)
         warm(4)
-        for n in range(1, len(steps)):
-            group_h(*steps[n - 1])
-            if n == 1:
-                dustbin_scores()
-                interleave_f(0, 0, "scalar", 1, 4)
-                interleave_f(0, 0, "scalar", 2, 4)
-            if n == 3:
-                quantize_f(0, 0)
-            if n >= 2:
-                scores(*steps[n - 2])
-            warm(3 if n >= 2 else 1)
+        widen(*steps[1], 1)
+        turn_h(*steps[1])
+        group_h(*steps[0])
+        dustbin_scores()
+        dustbin_turn()
+        interleave_f(0, 0, "scalar", 1, 4)
+        for n in range(2, len(steps)):
             widen(*steps[n], 1)
-            turn_h(*steps[n])
-            if n == 1:
-                dustbin_turn()
-                interleave_f(0, 0, "vector", 3, 4)
-            if n == 2:
+            if n == 3:
                 dustbin_column()
-            if n >= 2:
-                empty_scores(*steps[n - 2])
+            if n >= 3:
+                empty_scores(*steps[n - 3])
+            group_h(*steps[n - 1])
+            if n >= 4:
+                row_exp(*steps[n - 4])
+            if n == 2:
+                interleave_f(0, 0, "scalar", 2, 4)
+            if n == last:
+                turn_h(*steps[n])
+            scores(*steps[n - 2])
+            if n < last:
+                turn_h(*steps[n])
+            warm(3)
+            if n == 3:
+                interleave_f(0, 0, "vector", 3, 4)
             if n >= 3:
                 row_max(*steps[n - 3])
-                row_exp(*steps[n - 3])
         group_h(*steps[last])
+        row_exp(*steps[last - 3])
         scores(*steps[last - 1])
         warm(3)
-        empty_scores(*steps[last - 1])
-        row_max(*steps[last - 2])
+        quantize_f(0, 0)
+        empty_scores_and_max(*steps[last - 2])
         row_exp(*steps[last - 2])
         turn_scores(0, 0, 0)
-        turn_scores(0, 0, 1)
-        interleave_f(0, 1, "vector", 0, 2)
         scores(*steps[last])
         warm(3)
-        row_max(*steps[last - 1])
+        empty_scores_and_max(*steps[last - 1])
         row_exp(*steps[last - 1])
+        turn_scores(0, 0, 1)
         turn_scores(0, 1, 0)
         turn_scores(0, 1, 1)
-        turn_scores(1, 0, 0)
-        turn_scores(1, 0, 1)
         warm(4)
-        interleave_f(0, 1, "vector", 2, 4)
         empty_scores_and_max(*steps[last])
         row_exp(*steps[last])
         nc.scalar.activation(out=log_sum[:], in_=row_sum[:], func=ACT.Ln)
         interleave_f(1, 1, "scalar", 0, 2)
+        turn_scores(1, 0, 0)
+        turn_scores(1, 0, 1)
         turn_scores(1, 1, 0)
-        interleave_f(0, 1, "vector", 3, 4)
-        interleave_f(1, 0, "vector", 0, 2)
-        quantize_f(0, 1)
-        warm(4, f_codes[0][1], f_scales[0][1])
-        interleave_f(1, 0, "vector", 1, 2)
+        warm(4)
+        interleave_f(0, 1, "vector")
+        interleave_f(1, 0, "vector")
         nc.vector.tensor_tensor(out=lse[:], in0=log_sum[:], in1=neg_max[:], op=ALU.subtract)
-        interleave_f(1, 1, "vector", 1, 2)
+        quantize_f(0, 1)
         dust_partition_min()
         add_lse(0, 0, 0)
         add_lse(0, 1, 0)
@@ -550,7 +554,8 @@ def tile_saladsinkhorndustbinaggregation_w8_kernel(tc, h_bytes, h_scale, wp_word
         sum_upper()
         row_total(0, 4)
         total_upper()
-        row_inverse(0)
+        row_inverse(0, 0, 4)
+        row_inverse(0, 4, TILES)
         row_spread(0, (0, 5))
         row_sums(1, 0, 4, 4, TILES, TILES)
         nc.scalar.activation(out=inv_root[:], in_=ones[:, 0:1], func=ACT.Sqrt, scale=1.0 / E)
@@ -560,50 +565,52 @@ def tile_saladsinkhorndustbinaggregation_w8_kernel(tc, h_bytes, h_scale, wp_word
         warm(4)
         column_sum(0, 0, 0)
         column_sum(0, 0, 1)
-        column_sum(0, 1, 0)
         column_total(0, 0)
-        column_sum(0, 1, 1)
+        column_sum(0, 1, 0)
         column_factor(0, 0)
+        column_sum(0, 1, 1)
         column_total(0, 1)
+        interleave_f(1, 1, "scalar", 1, 2)
         gated(0, 0, 0, 2, 3)
-        column_factor(0, 1)
         row_total(1, TILES)
+        column_factor(0, 1)
         row_inverse(1)
         row_spread(1, (1, 2))
         warm(4)
         group_pg(0, 0, 0, 2)
         gated(0, 1, 0, 2, 6)
-        group_pg(0, 1, 0, 2)
         column_sum(1, 0, 0)
         aggregate(0, 0, 0, 2, 4)
-        square_sum(0, 0)
-        root(0, 0)
         column_sum(1, 0, 1)
-        column_sum(1, 1, 0)
         column_total(1, 0)
-        column_sum(1, 1, 1)
-        column_factor(1, 0)
-        column_total(1, 1)
-        aggregate(0, 1, 0, 2, 0)
+        group_pg(0, 1, 0, 2)
+        square_sum(0, 0)
+        column_sum(1, 1, 0)
         warm(4)
+        column_factor(1, 0)
+        column_sum(1, 1, 1)
+        column_total(1, 1)
+        warm_after(small["col2p", 1][:, 3:4])
+        root(0, 0)
+        gated(1, 0, 0, 2, 5)
         column_factor(1, 1)
+        group_pg(1, 0, 0, 2)
+        aggregate(0, 1, 0, 2, 0)
         square_sum(0, 1)
         root(0, 1)
-        gated(1, 0, 0, 2, 5)
-        group_pg(1, 0, 0, 2)
         gated(1, 1, 0, 1, 3)
         gated(1, 1, 1, 2, 6)
         warm(4)
         norm_factor(0, 0)
-        norm_factor(0, 1)
         normalise(0, 0, "scalar")
-        normalise(0, 1, "scalar")
         quantize_f(1, 1)
         aggregate(1, 0, 0, 2, 1)
         group_pg(1, 1, 0, 1, nc.vector.tensor_copy)
         group_pg(1, 1, 1, 2, nc.vector.tensor_copy)
         aggregate(1, 1, 0, 1, 2)
         aggregate(1, 1, 1, 2, 2)
+        norm_factor(0, 1)
+        normalise(0, 1, "vector")
         square_sum(1, 0)
         root(1, 0)
         square_sum(1, 1)

import math
from contextlib import ExitStack

import concourse.mybir as mybir
from concourse.masks import make_identity

B, S, H, C, E = 2, 1024, 512, 256, 512
FLOPS = 2 * B * S * H * C + 2 * B * C * S * E

F32 = mybir.dt.float32
BF16 = mybir.dt.bfloat16
U32 = mybir.dt.uint32
I32 = mybir.dt.int32
U8 = mybir.dt.uint8
FP8 = mybir.dt.float8_e4m3fn
FP8X4 = mybir.dt.float8_e4m3fn_x4
ALU = mybir.AluOpType
ACT = mybir.ActivationFunctionType
AX = mybir.AxisListType

P = 128
BANK = 512
TILES = S // P
GROUPS = S // 256
HALVES = C // P
PASSES = S // 512
SUM_N = 64
ROW = 264


def tile_saladsinkhorndustbinaggregation_w8_kernel(tc, h_bytes, h_scale, wp_words, wp_scales, z, g, f, out):
    nc = tc.nc
    with ExitStack() as ctx:
        keep = ctx.enter_context(tc.tile_pool(name="keep", bufs=1))
        stage = ctx.enter_context(tc.tile_pool(name="stage", bufs=4))
        psum = ctx.enter_context(tc.psum_pool(name="psum", bufs=1))
        ctx.enter_context(tc.manual_schedule())

        def bank(name, number):
            return psum.tile([P, BANK], F32, name=name, tag="bank_%d" % number)

        def kept(name, shape, dtype):
            return keep.tile(shape, dtype, name=name, align_bytes=64)

        both = range(B)
        ident = kept("ident", [P, P], F32)
        ones = kept("ones", [P, P], F32)
        inv_root = kept("inv_root", [P, 1], F32)
        z_rows = kept("z_rows", [P, P], BF16)
        neg_z_rows = kept("neg_z_rows", [P, P], F32)
        hs_cols = kept("hs_cols", [P, 4], F32)
        hs = kept("hs", [P, 2 * H], F32)
        h_first = kept("hbytes_first", [P, 1, 2 * H], U8)
        h_rest = kept("hbytes_rest", [P, GROUPS - 1, 2 * H], U8)
        h_second = kept("hbytes_second", [P, GROUPS, 2 * H], U8)
        hbytes = [[h_first[:, 0, :]] + [h_rest[:, q, :] for q in range(GROUPS - 1)], [h_second[:, q, :] for q in range(GROUPS)]]
        w_codes = kept("w_codes", [P, C], U32)
        w_scales = kept("w_scales", [P, C], U8)
        f_raw = [[kept("f_raw_%d_%d" % (b, a), [P, 4, E], BF16) for a in range(PASSES)] for b in both]
        f_codes = [[kept("f_codes_%d_%d" % (b, a), [P, E], U32) for a in range(PASSES)] for b in both]
        f_scales = [[kept("f_scales_%d_%d" % (b, a), [P, E], U8) for a in range(PASSES)] for b in both]
        gate = [kept("gate_%d" % b, [P, S], BF16) for b in both]
        neg_all = kept("neg_l", [P, B * TILES, ROW], F32)
        neg_l = [neg_all[:, b * TILES : (b + 1) * TILES, :] for b in both]
        dust_cost = kept("dust_cost", [P, B * TILES], F32)
        dust_exp = kept("dust_exp", [P, B * TILES], F32)
        dust_min_p = kept("dust_min_p", [P, B], F32)
        dust_min = kept("dust_min", [P, B], F32)
        dust_sum_p = kept("dust_sum_p", [P, B], F32)
        upper_sum = kept("upper_sum", [P, 4], F32)
        dust_inv = kept("dust_inv", [P, B], F32)
        neg_max = kept("neg_max", [P, B * TILES], F32)
        row_sum = kept("row_sum", [P, B * TILES], F32)
        log_sum = kept("log_sum", [P, B * TILES], F32)
        lse = kept("lse", [P, B * TILES], F32)
        cost = [[kept("cost_%d_%d" % (b, hf), [P, S], F32) for hf in range(HALVES)] for b in both]
        small = {}
        for b in both:
            for name, width in (("cmin", 4), ("col1", 2), ("v1", 2), ("dust", 8), ("row2", 8), ("u2", 8), ("col2p", 4), ("col2", 2),
                                ("v2", 2), ("ss", 2), ("ms", 2), ("rs", 2)):
                small[name, b] = kept("%s_%d" % (name, b), [P, width], F32)

        nc.sync.dma_start(out=hs_cols[:], in_=h_scale.rearrange("a o (p t) -> p (a o t)", t=4))

        def load_h(dst, b, q0, q1):
            rows = h_bytes[b, 256 * q0 : 256 * q1, :]
            nc.sync.dma_start(out=dst[:], in_=rows.rearrange("(q m e) k -> m q (e k)", m=P, e=2))

        def load_f(b, a):
            rows = f[b, 512 * a : 512 * (a + 1), :]
            nc.sync.dma_start(out=f_raw[b][a][:], in_=rows.rearrange("(p t) e -> p t e", t=4))

        nc.gpsimd.memset(w_scales[:].bitcast(I32), 0)
        make_identity(nc, ident[:])
        nc.gpsimd.memset(ones[:], 1.0)
        nc.gpsimd.memset(neg_z_rows[:], 0.0)

        load_h(h_first, 0, 0, 1)
        load_h(h_rest, 0, 1, GROUPS)
        nc.sync.dma_start(
            out=w_codes[:].bitcast(I32), in_=wp_words[0].rearrange("p n t -> p (n t)").bitcast(I32)
        )
        load_f(0, 0)
        for quad in range(4):
            nc.sync.dma_start(
                out=w_scales[32 * quad : 32 * quad + 4, :].bitcast(I32),
                in_=wp_scales[0, 4 * quad : 4 * quad + 4, :].bitcast(I32),
            )
        nc.sync.dma_start(out=z_rows[0 : B * TILES, :], in_=z.rearrange("b (j m) -> (b j) m", m=P))
        load_h(h_second, 1, 0, GROUPS)
        load_f(0, 1)
        load_f(1, 0)
        load_f(1, 1)
        for b in both:
            nc.sync.dma_start(out=gate[b][:], in_=g[b].partition_broadcast(P))

        held = {}
        def dustbin_scores():
            nc.scalar.activation(out=neg_z_rows[0 : B * TILES, :], in_=z_rows[0 : B * TILES, :], func=ACT.Copy, scale=-1.0)

        def dustbin_turn():
            z_bank = bank("z_bank", 4)
            nc.tensor.transpose(z_bank[:, 0:P], neg_z_rows[:], ident[:])
            held["z"] = z_bank

        def spread_scales():
            sb = bank("scale_bank", 5)
            for t in range(4):
                nc.tensor.transpose(sb[:, t * P : (t + 1) * P], hs_cols[:, t : t + 1].to_broadcast([P, P]), ident[:])
            nc.vector.tensor_copy(out=hs[:, 0:H].rearrange("p (n t) -> p n t", t=4), in_=sb[:].rearrange("p (t n) -> p n t", t=4))
            nc.scalar.copy(out=hs[:, H : 2 * H], in_=hs[:, 0:H])

        def dustbin_column():
            nc.vector.tensor_copy(out=neg_all[:, :, C], in_=held["z"][:, 0 : B * TILES])

        scratch = bank("scratch", 7)

        def warm_plain(count):
            for i in range(count):
                nc.tensor.matmul(out=scratch[:, 0:P], lhsT=ones[:], rhs=ident[:], start=True, stop=True)

        def warm_after(column):
            nc.tensor.matmul(out=scratch[:, 0:C], lhsT=ones[:], rhs=column.to_broadcast([P, C]), start=True, stop=True)

        def warm(count, codes=w_codes, scales=w_scales):
            for i in range(count):
                nc.tensor.matmul_mx(
                    out=scratch[:, 0:C], lhsT=w_codes[:, 0:P].bitcast(FP8X4), lhsT_scale=w_scales[:, 0:P],
                    rhs=codes[:, 0:C].bitcast(FP8X4), rhs_scale=scales[:, 0:C], start=True, stop=True,
                )


        def widen(b, q, pieces):
            hb = stage.tile([P, 2 * H], BF16, name="hb", align_bytes=64)
            width = 2 * H // pieces
            for e in range(pieces):
                cols = slice(e * width, (e + 1) * width)
                nc.vector.tensor_tensor(out=hb[:, cols], in0=hbytes[b][q][:, cols].bitcast(FP8), in1=hs[:, 0:width], op=ALU.mult)
            held["hb", b, q] = hb

        def turn_h(b, q):
            hb = held["hb", b, q]
            words = hb[:].bitcast(F32)
            turned = bank("turned", q % 2)
            for e in range(2):
                for u in range(2):
                    r = 2 * e + u
                    nc.tensor.transpose(turned[:, r * P : (r + 1) * P], words[:, 256 * e + u : 256 * (e + 1) : 2], ident[:])
            held["turned", b, q] = turned

        def group_h(b, q):
            turned = held["turned", b, q]
            grouped = stage.tile([P, 1024], BF16, name="grouped", align_bytes=64)
            nc.scalar.copy(
                out=grouped[:].bitcast(F32).rearrange("p (m r) -> p m r", r=4),
                in_=turned[:].rearrange("p (r m) -> p m r", r=4),
            )
            held["grouped", b, q] = grouped

        def scores(b, q):
            codes = stage.tile([P, 256], U32, name="h_codes", align_bytes=64)
            scales = stage.tile([P, 256], U8, name="h_scales", align_bytes=64)
            nc.vector.quantize_mx(out=codes[:].bitcast(FP8X4), scales=scales[:], in_=held["grouped", b, q][:])
            t_bank = bank("t_bank", 2 + q % 2)
            for i in range(2):
                cols = slice(i * P, (i + 1) * P)
                nc.tensor.matmul_mx(
                    out=t_bank[:, i * C : (i + 1) * C],
                    lhsT=codes[:, cols].bitcast(FP8X4),
                    lhsT_scale=scales[:, cols],
                    rhs=w_codes[:].bitcast(FP8X4),
                    rhs_scale=w_scales[:],
                    start=True,
                    stop=True,
                )
            held["t", b, q] = t_bank

        def empty_scores(b, q):
            t_bank = held["t", b, q]
            nc.scalar.activation(
                out=neg_l[b][:, 2 * q : 2 * q + 2, 0:C], in_=t_bank[:].rearrange("p (i c) -> p i c", i=2), func=ACT.Copy, scale=-1.0
            )

        def row_max(b, q):
            n = b * TILES + 2 * q
            nc.vector.tensor_reduce(
                out=neg_max[:, n : n + 2], in_=neg_l[b][:, 2 * q : 2 * q + 2, 0 : C + 1], axis=AX.X, op=ALU.min
            )

        def empty_scores_and_max(b, q):
            for i in range(2):
                j = 2 * q + i
                n = b * TILES + j
                nc.vector.tensor_scalar(
                    out=neg_l[b][:, j, 0:C], in0=held["t", b, q][:, i * C : (i + 1) * C], scalar1=-1.0,
                    scalar2=neg_l[b][:, j, C : C + 1], op0=ALU.mult, op1=ALU.min, accum_out=neg_max[:, n : n + 1],
                )

        def row_exp(b, q):
            for j in (2 * q, 2 * q + 1):
                n = b * TILES + j
                junk = stage.tile([P, C + 1], BF16, name="junk_row")
                nc.scalar.activation(
                    out=junk[:], in_=neg_l[b][:, j, 0 : C + 1], func=ACT.Exp, scale=-1.0, bias=neg_max[:, n : n + 1],
                    accum_out=row_sum[:, n : n + 1],
                )

        def interleave_f(b, a, engine, part=0, parts=1):
            if part == 0:
                held["fi", b, a] = kept("f_grouped_%d_%d" % (b, a), [P, E, 4], BF16)
            cols = slice(part * E // parts, (part + 1) * E // parts)
            dst = held["fi", b, a][:, cols, :].rearrange("p (c i) t -> p c t i", i=4)
            src = f_raw[b][a][:, :, cols].rearrange("p t (c i) -> p c t i", i=4)
            if engine == "scalar":
                nc.scalar.copy(out=dst, in_=src)
            else:
                nc.vector.tensor_copy(out=dst, in_=src)

        def quantize_f(b, a):
            nc.vector.quantize_mx(
                out=f_codes[b][a][:].bitcast(FP8X4), scales=f_scales[b][a][:],
                in_=held["fi", b, a][:].rearrange("p c t -> p (c t)"),
            )

        def cost_bank_number(b, k, hf):
            return (4, 5, 6, 0, 1, 2, 3, 6)[4 * b + 2 * k + hf]

        def turn_scores(b, k, hf):
            nb = bank("cost_bank", cost_bank_number(b, k, hf))
            for jj in range(4):
                nc.tensor.matmul(
                    out=nb[:, jj * P : (jj + 1) * P], lhsT=neg_l[b][:, 4 * k + jj, hf * P : (hf + 1) * P], rhs=ident[:],
                    is_transpose=True, start=(jj == 0), stop=False,
                )
            held["n", b, k, hf] = nb

        def add_lse(b, k, hf):
            nb = held["n", b, k, hf]
            for jj in range(4):
                n = b * TILES + 4 * k + jj
                nc.tensor.matmul(
                    out=nb[:, jj * P : (jj + 1) * P], lhsT=lse[:, n : n + 1].to_broadcast([P, P]), rhs=ident[:],
                    is_transpose=(jj > 0 or (k, hf) == (0, 0)), start=False, stop=(jj == 3),
                )

        def column_min(b, k, hf):
            cmin = small["cmin", b]
            nc.vector.tensor_scalar(
                out=cost[b][hf][:, k * BANK : (k + 1) * BANK], in0=held["n", b, k, hf][:], scalar1=1.0,
                scalar2=(None if k == 0 else cmin[:, hf : hf + 1]), op0=ALU.mult, op1=ALU.min,
                accum_out=cmin[:, 2 * k + hf : 2 * k + hf + 1],
            )

        def dust_partition_min():
            nc.vector.tensor_tensor(out=dust_cost[:], in0=lse[:], in1=neg_all[:, :, C], op=ALU.add)

        def dust_partition_min2():
            nc.vector.tensor_reduce(out=dust_min_p[:], in_=dust_cost[:].rearrange("p (b j) -> p b j", b=B), axis=AX.X, op=ALU.min)

        def dust_spread(number):
            db = bank("dust_bank", number)
            for b in both:
                nc.tensor.transpose(db[:, b * P : (b + 1) * P], dust_min_p[:, b : b + 1].to_broadcast([P, P]), ident[:])
            held["dust"] = db

        def dust_weights_min():
            nc.vector.tensor_reduce(
                out=dust_min[:], in_=held["dust"][:, 0 : B * P].rearrange("p (b m) -> p b m", b=B), axis=AX.X, op=ALU.min
            )

        def dust_weights():
            for b in both:
                cols = slice(b * TILES, (b + 1) * TILES)
                nc.scalar.activation(
                    out=dust_exp[:, cols], in_=dust_cost[:, cols], func=ACT.Exp, scale=-1.0, bias=dust_min[:, b : b + 1],
                    accum_out=dust_sum_p[:, b : b + 1],
                )

        def dust_total(number):
            db = bank("dust_sum_bank", number)
            nc.tensor.matmul(out=db[:, 0:B], lhsT=ones[:], rhs=dust_sum_p[:], start=True, stop=True)
            held["dust"] = db

        def dust_mass():
            nc.vector.reciprocal(out=dust_inv[:], in_=held["dust"][:, 0:B])
            for b in both:
                nc.gpsimd.tensor_scalar(
                    out=small["dust", b][:], in0=dust_exp[:, b * TILES : (b + 1) * TILES], scalar1=dust_inv[:, b : b + 1],
                    scalar2=float(S - C), op0=ALU.mult, op1=ALU.mult,
                )

        def column_exp(b, hf):
            nc.scalar.activation(
                out=cost[b][hf][:], in_=cost[b][hf][:], func=ACT.Exp, scale=-1.0,
                bias=small["cmin", b][:, 2 + hf : 3 + hf], accum_out=small["col1", b][:, hf : hf + 1],
            )

        def column_inverse(b, hf):
            nc.vector.reciprocal(out=small["v1", b][:, hf : hf + 1], in_=small["col1", b][:, hf : hf + 1])

        def row_sums(b, hf, number, j0, j1, tiles):
            if hf == 0 and j0 == 0:
                held["rows", b] = bank("row_bank", number)
            for j in range(j0, j1):
                nc.tensor.matmul(
                    out=held["rows", b][:, j * SUM_N : (j + 1) * SUM_N], lhsT=cost[b][hf][:, j * P : (j + 1) * P],
                    rhs=small["v1", b][:, hf : hf + 1].to_broadcast([P, SUM_N]),
                    start=(hf == 0 and j == 0), stop=(hf == HALVES - 1 and j == tiles - 1),
                )

        def row_total(b, tiles):
            nc.vector.tensor_tensor(
                out=small["row2", b][:, 0:tiles], in0=held["rows", b][:, 0 : tiles * SUM_N : SUM_N],
                in1=small["dust", b][:, 0:tiles], op=ALU.add,
            )

        def scale_upper(hf):
            upper = cost[0][hf][:, BANK:S]
            nc.vector.tensor_scalar(out=upper, in0=upper, scalar1=small["v1", 0][:, hf : hf + 1], scalar2=None, op0=ALU.mult)

        def turn_upper(hf, number):
            if hf == 0:
                held["upper"] = bank("upper_bank", number)
            for jj in range(4):
                nc.tensor.matmul(
                    out=held["upper"][:, jj * P : (jj + 1) * P], lhsT=cost[0][hf][:, BANK + jj * P : BANK + (jj + 1) * P],
                    rhs=ident[:], is_transpose=True, start=(hf == 0 and jj == 0), stop=(hf == HALVES - 1 and jj == 3),
                )

        def sum_upper():
            nc.vector.tensor_reduce(
                out=upper_sum[:], in_=held["upper"][:].rearrange("p (j c) -> p j c", j=4), axis=AX.X, op=ALU.add
            )

        def total_upper():
            nc.vector.tensor_tensor(out=small["row2", 0][:, 4:TILES], in0=upper_sum[:], in1=small["dust", 0][:, 4:TILES], op=ALU.add)

        def row_inverse(b, j0=0, j1=TILES):
            nc.vector.reciprocal(out=small["u2", b][:, j0:j1], in_=small["row2", b][:, j0:j1])

        def row_spread(b, numbers):
            for k in range(2):
                ub = bank("u_bank", numbers[k])
                for jj in range(4):
                    j = 4 * k + jj
                    nc.tensor.transpose(ub[:, jj * P : (jj + 1) * P], small["u2", b][:, j : j + 1].to_broadcast([P, P]), ident[:])
                held["u", b, k] = ub

        def column_sum(b, hf, k):
            cols = slice(k * BANK, (k + 1) * BANK)
            nc.vector.scalar_tensor_tensor(
                out=cost[b][hf][:, cols], in0=cost[b][hf][:, cols],
                scalar=(1.0 if (b, k) == (0, 1) else small["v1", b][:, hf : hf + 1]), in1=held["u", b, k][:], op0=ALU.mult, op1=ALU.mult,
                accum_out=small["col2p", b][:, 2 * hf + k : 2 * hf + k + 1],
            )

        def column_total(b, hf):
            halves = stage.tile([P, 2], F32, name="junk_total")
            nc.scalar.activation(
                out=halves[:], in_=small["col2p", b][:, 2 * hf : 2 * hf + 2], func=ACT.Copy, scale=1.0 / math.sqrt(S),
                accum_out=small["col2", b][:, hf : hf + 1],
            )

        def column_factor(b, hf):
            nc.vector.reciprocal(out=small["v2", b][:, hf : hf + 1], in_=small["col2", b][:, hf : hf + 1])

        def gated(b, hf, a0, a1, number):
            n = a1 - a0
            pg = stage.tile([P, n * 512], BF16, name="pg", align_bytes=64)
            cols = slice(512 * a0, 512 * a1)
            nc.vector.scalar_tensor_tensor(
                out=pg[:], in0=cost[b][hf][:, cols], scalar=small["v2", b][:, hf : hf + 1], in1=gate[b][:, cols],
                op0=ALU.mult, op1=ALU.mult,
            )
            words = pg[:].bitcast(F32)
            turned = bank("pg_turned", number)
            for a in range(n):
                for u in range(2):
                    r = 2 * a + u
                    nc.tensor.transpose(turned[:, r * P : (r + 1) * P], words[:, 256 * a + u : 256 * (a + 1) : 2], ident[:])
            held["pg_turned", b, hf, a0] = turned

        def group_pg(b, hf, a0, a1, copy=nc.scalar.copy):
            n = a1 - a0
            turned = held["pg_turned", b, hf, a0]
            grouped = stage.tile([P, n * 512], BF16, name="pg_grouped", align_bytes=64)
            copy(
                out=grouped[:].bitcast(F32).rearrange("p (a c u) -> p a c u", a=n, u=2),
                in_=turned[:, 0 : n * 256].rearrange("p (a u c) -> p a c u", a=n, u=2),
            )
            held["pg", b, hf, a0] = grouped

        def aggregate(b, hf, a0, a1, number):
            n = a1 - a0
            codes = stage.tile([P, n * P], U32, name="pg_codes", align_bytes=64)
            scales = stage.tile([P, n * P], U8, name="pg_scales", align_bytes=64)
            nc.vector.quantize_mx(out=codes[:].bitcast(FP8X4), scales=scales[:], in_=held["pg", b, hf, a0][:])
            if a0 == 0:
                held["v", b, hf] = bank("v_bank", number)
            for a in range(a0, a1):
                cols = slice((a - a0) * P, (a - a0 + 1) * P)
                nc.tensor.matmul_mx(
                    out=held["v", b, hf][:], lhsT=codes[:, cols].bitcast(FP8X4), lhsT_scale=scales[:, cols],
                    rhs=f_codes[b][a][:].bitcast(FP8X4), rhs_scale=f_scales[b][a][:],
                    start=(a == 0), stop=(a == PASSES - 1),
                )

        def square_sum(b, hf):
            junk = stage.tile([P, E], BF16, name="junk_sq")
            col = slice(hf, hf + 1)
            nc.scalar.activation(out=junk[:], in_=held["v", b, hf][:], func=ACT.Square, scale=inv_root[:], accum_out=small["ss", b][:, col])

        def root(b, hf):
            col = slice(hf, hf + 1)
            nc.scalar.activation(out=small["ms", b][:, col], in_=small["ss", b][:, col], func=ACT.Sqrt, bias=1e-6)

        def norm_factor(b, hf):
            nc.vector.reciprocal(out=small["rs", b][:, hf : hf + 1], in_=small["ms", b][:, hf : hf + 1])

        def normalise(b, hf, engine, part=0, parts=1):
            cols = slice(part * E // parts, (part + 1) * E // parts)
            y = kept("y_%d_%d_%d" % (b, hf, part), [P, E // parts], F32)
            rs = small["rs", b][:, hf : hf + 1]
            if engine == "scalar":
                nc.scalar.activation(out=y[:], in_=held["v", b, hf][:, cols], func=ACT.Copy, scale=rs)
            else:
                nc.vector.tensor_scalar(out=y[:], in0=held["v", b, hf][:, cols], scalar1=rs, scalar2=None, op0=ALU.mult)
            nc.sync.dma_start(out=out[b, hf * P : (hf + 1) * P, cols], in_=y[:])

        steps = [(b, q) for b in both for q in range(GROUPS)]
        last = len(steps) - 1
        banks4 = [(k, hf) for k in range(2) for hf in range(HALVES)]

        spread_scales()
        warm_plain(4)
        widen(0, 0, 2)
        turn_h(0, 0)
        interleave_f(0, 0, "scalar", 0, 4)
        warm(4)
        widen(*steps[1], 1)
        turn_h(*steps[1])
        group_h(*steps[0])
        dustbin_scores()
        dustbin_turn()
        interleave_f(0, 0, "scalar", 1, 4)
        for n in range(2, len(steps)):
            widen(*steps[n], 1)
            if n == 3:
                dustbin_column()
            if n >= 3:
                empty_scores(*steps[n - 3])
            group_h(*steps[n - 1])
            if n >= 4:
                row_exp(*steps[n - 4])
            if n == 2:
                interleave_f(0, 0, "scalar", 2, 4)
            if n == last:
                turn_h(*steps[n])
            scores(*steps[n - 2])
            if n < last:
                turn_h(*steps[n])
            warm(3)
            if n == 3:
                interleave_f(0, 0, "vector", 3, 4)
            if n >= 3:
                row_max(*steps[n - 3])
        group_h(*steps[last])
        row_exp(*steps[last - 3])
        scores(*steps[last - 1])
        warm(3)
        quantize_f(0, 0)
        empty_scores_and_max(*steps[last - 2])
        row_exp(*steps[last - 2])
        turn_scores(0, 0, 0)
        scores(*steps[last])
        warm(3)
        empty_scores_and_max(*steps[last - 1])
        row_exp(*steps[last - 1])
        turn_scores(0, 0, 1)
        turn_scores(0, 1, 0)
        turn_scores(0, 1, 1)
        warm(4)
        empty_scores_and_max(*steps[last])
        row_exp(*steps[last])
        nc.scalar.activation(out=log_sum[:], in_=row_sum[:], func=ACT.Ln)
        interleave_f(1, 1, "scalar", 0, 2)
        turn_scores(1, 0, 0)
        turn_scores(1, 0, 1)
        turn_scores(1, 1, 0)
        warm(4)
        interleave_f(0, 1, "vector")
        interleave_f(1, 0, "vector")
        nc.vector.tensor_tensor(out=lse[:], in0=log_sum[:], in1=neg_max[:], op=ALU.subtract)
        quantize_f(0, 1)
        dust_partition_min()
        add_lse(0, 0, 0)
        add_lse(0, 1, 0)
        add_lse(0, 0, 1)
        column_min(0, 0, 0)
        dust_partition_min2()
        add_lse(0, 1, 1)
        dust_spread(4)
        column_min(0, 1, 0)
        column_exp(0, 0)
        add_lse(1, 0, 0)
        add_lse(1, 1, 0)
        add_lse(1, 0, 1)
        turn_scores(1, 1, 1)
        add_lse(1, 1, 1)
        column_min(0, 0, 1)
        dust_weights_min()
        column_min(0, 1, 1)
        column_exp(0, 1)
        dust_weights()
        column_inverse(0, 0)
        row_sums(0, 0, 5, 0, 4, 4)
        column_min(1, 0, 0)
        scale_upper(0)
        turn_upper(0, 0)
        column_min(1, 1, 0)
        column_exp(1, 0)
        column_inverse(0, 1)
        dust_total(4)
        row_sums(0, 1, 5, 0, 2, 4)
        scale_upper(1)
        turn_upper(1, 0)
        row_sums(0, 1, 5, 2, 4, 4)
        column_min(1, 0, 1)
        dust_mass()
        column_min(1, 1, 1)
        column_exp(1, 1)
        column_inverse(1, 0)
        row_sums(1, 0, 4, 0, 4, TILES)
        sum_upper()
        row_total(0, 4)
        total_upper()
        row_inverse(0, 0, 4)
        row_inverse(0, 4, TILES)
        row_spread(0, (0, 5))
        row_sums(1, 0, 4, 4, TILES, TILES)
        nc.scalar.activation(out=inv_root[:], in_=ones[:, 0:1], func=ACT.Sqrt, scale=1.0 / E)
        quantize_f(1, 0)
        column_inverse(1, 1)
        row_sums(1, 1, 4, 0, TILES, TILES)
        warm(4)
        column_sum(0, 0, 0)
        column_sum(0, 0, 1)
        column_total(0, 0)
        column_sum(0, 1, 0)
        column_factor(0, 0)
        column_sum(0, 1, 1)
        column_total(0, 1)
        interleave_f(1, 1, "scalar", 1, 2)
        gated(0, 0, 0, 2, 3)
        row_total(1, TILES)
        column_factor(0, 1)
        row_inverse(1)
        row_spread(1, (1, 2))
        warm(4)
        group_pg(0, 0, 0, 2)
        gated(0, 1, 0, 2, 6)
        column_sum(1, 0, 0)
        aggregate(0, 0, 0, 2, 4)
        column_sum(1, 0, 1)
        column_total(1, 0)
        group_pg(0, 1, 0, 2)
        square_sum(0, 0)
        column_sum(1, 1, 0)
        warm(4)
        column_factor(1, 0)
        column_sum(1, 1, 1)
        column_total(1, 1)
        warm_after(small["col2p", 1][:, 3:4])
        root(0, 0)
        gated(1, 0, 0, 2, 5)
        column_factor(1, 1)
        group_pg(1, 0, 0, 2)
        aggregate(0, 1, 0, 2, 0)
        square_sum(0, 1)
        root(0, 1)
        gated(1, 1, 0, 1, 3)
        gated(1, 1, 1, 2, 6)
        warm(4)
        norm_factor(0, 0)
        normalise(0, 0, "scalar")
        quantize_f(1, 1)
        aggregate(1, 0, 0, 2, 1)
        group_pg(1, 1, 0, 1, nc.vector.tensor_copy)
        group_pg(1, 1, 1, 2, nc.vector.tensor_copy)
        aggregate(1, 1, 0, 1, 2)
        aggregate(1, 1, 1, 2, 2)
        norm_factor(0, 1)
        normalise(0, 1, "vector")
        square_sum(1, 0)
        root(1, 0)
        square_sum(1, 1)
        root(1, 1)
        norm_factor(1, 0)
        normalise(1, 0, "vector")
        norm_factor(1, 1)
        normalise(1, 1, "vector", 0, 2)
        normalise(1, 1, "vector", 1, 2)
